import numpy as np
import ml_dtypes


def mxq(x, axis, fmt="e4m3"):
    dtype, down = {"e4m3": (ml_dtypes.float8_e4m3fn, 7), "e5m2": (ml_dtypes.float8_e5m2, 14)}[fmt]
    v = np.moveaxis(np.asarray(x, np.float32).astype(ml_dtypes.bfloat16).astype(np.float64), axis, -1)
    blocks = v.reshape(v.shape[:-1] + (-1, 32))
    amax = np.abs(blocks).max(-1, keepdims=True)
    byte = np.maximum(np.where(amax > 0, np.frexp(amax)[1] - 1 + 127, 0) - down, 1)
    scale = np.exp2(byte - 127.0)
    codes = (blocks / scale).astype(np.float32).astype(dtype).astype(np.float64)
    return np.moveaxis((codes * scale).reshape(v.shape), -1, axis)


WIDE = False


def mx_kscale(k):
    if not WIDE:
        return np.ones(k)
    levels = np.array([10, -10, 5, -5, 0])
    if k % 512:
        return np.exp2(np.random.permutation(np.resize(levels, k // 32))).repeat(32)
    a = np.empty((k // 512, 16))
    for p in range(k // 512):
        a[p, :8] = np.random.permutation(np.resize(levels, 8))
        for g in range(8):
            far = levels[np.abs(levels - a[p, g]) >= 10]
            a[p, g + 8] = far[np.random.randint(len(far))]
    return np.exp2(a.ravel()).repeat(32)


def f64(x):
    return np.asarray(x).astype(np.float64)


def striped(idx):
    return np.tile(idx.reshape(-1, 16).T, (8, 1)).astype(np.uint16)


def unstriped(offs):
    return offs[:16].T.reshape(-1).astype(np.int64)


E2M1 = np.array([0.0, 0.5, 1.0, 1.5, 2.0, 3.0, 4.0, 6.0, -0.0, -0.5, -1.0, -1.5, -2.0, -3.0, -4.0, -6.0])


def pack_weight(w, fmt):
    k, n = w.shape
    w = f64(np.asarray(w, np.float32).astype(ml_dtypes.bfloat16)).reshape(k // 32, 32, n)
    amax = np.abs(w).max(1)
    if fmt == "e4m3":
        byte = np.frexp(amax)[1] - 1 + 127 - 7
    else:
        mant, ex = np.frexp(amax / 6.0)
        byte = np.where(mant > 0.5, ex, ex - 1) + 127
    byte = np.clip(np.where(amax > 0, byte, 1), 1, 254)
    scaled = (w * np.exp2(127.0 - byte)[:, None, :]).reshape(k, n).astype(np.float32)
    by_word = np.ascontiguousarray(scaled.reshape(k // 512, 128, 4, n).transpose(0, 1, 3, 2))
    if fmt == "e4m3":
        words = by_word.astype(ml_dtypes.float8_e4m3fn).view(np.uint8)
    else:
        c = by_word.astype(ml_dtypes.float4_e2m1fn).view(np.uint8) & 0xF
        words = (c[..., 0::2] | (c[..., 1::2] << 4)).reshape(k // 512, 128, 2 * n)
    return np.ascontiguousarray(words), np.ascontiguousarray(byte.astype(np.uint8).reshape(k // 512, 16, n))


def unpack_weight(words, scales, fmt):
    g, _, n = scales.shape
    words = np.ascontiguousarray(words).reshape(g, 128, n, -1)
    if fmt == "e4m3":
        vals = words.view(ml_dtypes.float8_e4m3fn).astype(np.float64)
    else:
        nib = np.empty((g, 128, n, 4), np.uint8)
        nib[..., 0::2] = words & 0xF
        nib[..., 1::2] = words >> 4
        vals = E2M1[nib]
    vals = vals * np.repeat(np.exp2(scales.astype(np.float64) - 127.0), 8, axis=1)[..., None]
    return vals.transpose(0, 1, 3, 2).reshape(g * 512, n)


def planes(y):
    n, m = y.shape
    v = y.astype(np.float32).astype(ml_dtypes.bfloat16).astype(np.float64).reshape(n // 32, 32, m)
    top = np.abs(v).max(1)
    byte = np.clip(np.where(top > 0, np.frexp(top)[1] - 1 + 127 - 7, 1), 1, 254)
    codes = (v * np.exp2(127.0 - byte)[:, None, :]).reshape(n, m).astype(np.float32).astype(ml_dtypes.float8_e4m3fn).view(np.uint8)
    words = codes.reshape(n // 512, 128, 4, m).transpose(0, 1, 3, 2)
    return np.ascontiguousarray(words), np.ascontiguousarray(byte.astype(np.uint8).reshape(n // 512, 16, m))


def relu2(v):
    return np.maximum(v, 0.0) ** 2


K, T, E, C, H, HS, N = 512, 512, 8, 128, 512, 1024, 512


def by_expert(wq, xq):
    return np.concatenate([wq[e].T @ xq[:, e * C:(e + 1) * C] for e in range(E)], axis=1)


def setup_inputs():
    n = np.random.standard_normal
    s = mx_kscale(K)
    u = mx_kscale(H)
    v = mx_kscale(HS)
    first = np.random.permutation(np.repeat(np.arange(E), T // E))
    second = (first + 1 + np.random.permutation(np.repeat(np.arange(E - 1), -(-T // (E - 1)))[:T])) % E
    while np.bincount(second, minlength=E).max() != T // E:
        load = np.bincount(second, minlength=E); hi, lo = int(load.argmax()), int(load.argmin())
        t = np.flatnonzero((second == hi) & (first != lo))[0]; second[t] = lo
    slot_token = np.empty(E * C, np.int64); pos = np.empty((2, T), np.int64); fill = np.zeros(E, np.int64)
    place = np.stack([np.random.permutation(C) for _ in range(E)])
    for r, deal in enumerate((first, second)):
        for t in np.random.permutation(T):
            e = deal[t]; j = e * C + place[e, fill[e]]; fill[e] += 1; slot_token[j] = t; pos[r, t] = j
    g = np.random.uniform(0.2, 0.8, T)
    x = pack_weight(n((K, T)) * s[:, None], "e4m3")
    w1 = [pack_weight(m, "e2m1") for m in n((E, K, H)) / np.sqrt(K) / s[None, :, None] * u]
    w2 = [pack_weight(m, "e2m1") for m in n((E, H, N)) / np.sqrt(H) / u[None, :, None] ** 2]
    w1s = pack_weight(n((K, HS)) / np.sqrt(K) / s[:, None] * v, "e4m3")
    w2s = pack_weight(n((HS, N)) / np.sqrt(HS) / v[:, None] ** 2, "e4m3")
    return {
        "x_words": x[0],
        "x_scales": x[1],
        "w1_words": np.stack([m[0] for m in w1]),
        "w1_scales": np.stack([m[1] for m in w1]),
        "w2_words": np.stack([m[0] for m in w2]),
        "w2_scales": np.stack([m[1] for m in w2]),
        "w1s_words": w1s[0],
        "w1s_scales": w1s[1],
        "w2s_words": w2s[0],
        "w2s_scales": w2s[1],
        "gate": np.stack([np.tile(g, (128, 1)), np.tile(1.0 - g, (128, 1))]).astype(np.float32),
        "offs": striped(slot_token),
        "pos1": striped(pos[0]),
        "pos2": striped(pos[1]),
    }


def reference(x_words, x_scales, w1_words, w1_scales, w2_words, w2_scales, w1s_words, w1s_scales, w2s_words, w2s_scales, gate, offs, pos1, pos2):
    w1 = np.stack([unpack_weight(w1_words[e], w1_scales[e], "e2m1") for e in range(E)])
    w2 = np.stack([unpack_weight(w2_words[e], w2_scales[e], "e2m1") for e in range(E)])
    w1s = unpack_weight(w1s_words, w1s_scales, "e4m3")
    w2s = unpack_weight(w2s_words, w2s_scales, "e4m3")
    idx = unstriped(offs)
    x = unpack_weight(x_words, x_scales, "e4m3")
    hs = relu2(w1s.T @ x)
    ys = w2s.T @ mxq(hs, 0, "e4m3")
    h = relu2(by_expert(w1, x[:, idx]))
    y = by_expert(w2, mxq(h, 0, "e4m3"))
    c = sum(f64(gate[r, :1]) * y[:, unstriped(p)] for r, p in enumerate((pos1, pos2)))
    out_0 = ys + c
    return (out_0,) + planes(out_0)

@@ -1,0 +1,241 @@
+from contextlib import ExitStack
+
+import concourse.mybir as mybir
+from concourse.masks import make_identity
+
+K, T, E, C, H, HS, N = 512, 512, 8, 128, 512, 1024, 512
+FLOPS = 2 * (E * C * (K * H + H * N) + T * (K * HS + HS * N))
+
+F32 = mybir.dt.float32
+BF16 = mybir.dt.bfloat16
+I32 = mybir.dt.int32
+U32 = mybir.dt.uint32
+U16 = mybir.dt.uint16
+U8 = mybir.dt.uint8
+FP8X4 = mybir.dt.float8_e4m3fn_x4
+FP4X4 = mybir.dt.float4_e2m1fn_x4
+ACT = mybir.ActivationFunctionType
+ALU = mybir.AluOpType
+
+P = 128
+PACK = 4
+QUADS = 4
+PASS = P * PACK
+SLOTS = E * C
+ROW_BLOCKS = N // P
+TOKEN_TILES = T // P
+SHARED_PASSES = HS // PASS
+LIST_ROWS = 16
+W1_GROUPS = [1,1,2,4]
+VECTOR_RELU_EXPERTS = [4,5,6,7]
+VECTOR_RELU_SHARED = [0,1]
+VECTOR_SQUARE_SHARED = []
+SHARED_BANKS = [[6,7],[6,7],[0,2],[1,3],[0,2],[1,3],[0,6],[1,7]]
+YS_BANKS = [3,2,4,5]
+TOKEN_BANKS = [0,1,0,1]
+BACK_BANKS = [6,7,6,7]
+PRE_BANKS = [0,1,0,1,0,1,0,1]
+TURN_BANKS = [2,3,2,3,2,3,2,3]
+Y_BANKS = [4,5,4,5,4,5,4,5]
+
+
+def tile_moe_shf_mlp_relu2_kernel(
+    tc, x_words, x_scales, w1_words, w1_scales, w2_words, w2_scales, w1s_words, w1s_scales,
+    w2s_words, w2s_scales, gate, offs, pos1, pos2, out_0, out_1, out_2,
+):
+    nc = tc.nc
+    with ExitStack() as ctx:
+        keep = ctx.enter_context(tc.tile_pool(name="keep", bufs=1))
+        psum = ctx.enter_context(tc.psum_pool(name="psum", bufs=1))
+
+        def held(name, shape, dtype):
+            return keep.tile(shape, dtype, name=name, align_bytes=64)
+
+        banks = [psum.tile([P, PASS], F32, name="bank%d" % i) for i in range(8)]
+
+        def load_scale_rows(queue, plane, scales):
+            for q in range(QUADS):
+                queue.dma_start(
+                    out=plane[32 * q : 32 * q + 4, :, :].bitcast(I32),
+                    in_=scales[:, 4 * q : 4 * q + 4, :].rearrange("g r n -> r g n").bitcast(I32),
+                )
+
+        offs_sb = keep.tile([P, SLOTS // LIST_ROWS], U16, name="offs_sb")
+        pos_sb = [keep.tile([P, T // LIST_ROWS], U16, name="pos%d_sb" % r) for r in range(2)]
+        x_sb = held("x_sb", [P, T], I32)
+        x_plane = held("x_plane", [P, 1, T], U8)
+        w1_plane = held("w1_plane", [P, E, H], U8)
+        w2_plane = held("w2_plane", [P, E, N], U8)
+        w1s_plane = held("w1s_plane", [P, 1, HS], U8)
+        w2s_plane = held("w2s_plane", [P, SHARED_PASSES, N], U8)
+        w1_sb = [held("w1_sb%d" % i, [P, n, 2 * H], U8) for i, n in enumerate(W1_GROUPS)]
+        w1_of = [w1_sb[i][:, m, :] for i, n in enumerate(W1_GROUPS) for m in range(n)]
+        w2_sb = [held("w2_sb%d" % i, [P, 4, 2 * N], U8) for i in range(E // 4)]
+        w1s_sb = [held("w1s_sb%d" % g, [P, PASS], I32) for g in range(SHARED_PASSES)]
+        w2s_sb = held("w2s_sb", [P, SHARED_PASSES, N], I32)
+        gate_sb = held("gate_sb", [P, 2, T], F32)
+        ident = held("ident", [P, P], F32)
+
+        nc.gpsimd.memset(x_plane[:].bitcast(I32), 0)
+        nc.vector.memset(w1_plane[:].bitcast(I32), 0)
+        make_identity(nc, ident[:])
+        nc.gpsimd.memset(w1s_plane[:].bitcast(I32), 0)
+        nc.gpsimd.memset(w2_plane[:].bitcast(I32), 0)
+        nc.gpsimd.memset(w2s_plane[:].bitcast(I32), 0)
+        warm = held("warm", [P, 1], F32)
+        nc.scalar.activation(out=warm[:], in_=ident[:, 0:1], func=ACT.Square)
+
+        def load_experts(queue, tile, words, first, count):
+            queue.dma_start(
+                out=tile[:].bitcast(I32),
+                in_=words[first : first + count, 0].rearrange("e p n -> p e n").bitcast(I32),
+            )
+
+        w1s_flat = w1s_words[0].rearrange("p l d -> p (l d)").bitcast(I32)
+        nc.sync.dma_start(offs_sb[:], offs)
+        load_scale_rows(nc.sync, x_plane, x_scales)
+        nc.sync.dma_start(out=x_sb[:], in_=x_words[0].rearrange("p t d -> p (t d)").bitcast(I32))
+        load_experts(nc.sync, w1_sb[0], w1_words, 0, 1)
+        load_scale_rows(nc.sync, w1_plane, w1_scales[:, 0])
+        load_experts(nc.sync, w1_sb[1], w1_words, 1, 1)
+        load_experts(nc.sync, w1_sb[2], w1_words, 2, 2)
+        load_experts(nc.sync, w1_sb[3], w1_words, 4, 4)
+        load_scale_rows(nc.sync, w2_plane, w2_scales[:, 0])
+        load_experts(nc.sync, w2_sb[0], w2_words, 0, 4)
+        load_experts(nc.sync, w2_sb[1], w2_words, 4, 4)
+        nc.sync.dma_start(pos_sb[0][:], pos1)
+        nc.sync.dma_start(pos_sb[1][:], pos2)
+        nc.sync.dma_start(out=gate_sb[:], in_=gate.rearrange("r p t -> p r t"))
+        load_scale_rows(nc.sync, w1s_plane, w1s_scales)
+        nc.sync.dma_start(out=w1s_sb[0][:], in_=w1s_flat[:, 0:PASS])
+        nc.sync.dma_start(out=w1s_sb[1][:], in_=w1s_flat[:, PASS : 2 * PASS])
+        load_scale_rows(nc.sync, w2s_plane, w2s_scales)
+        nc.sync.dma_start(out=w2s_sb[:], in_=w2s_words.rearrange("g p n d -> p g (n d)").bitcast(I32))
+
+        def hidden(tokens, token_scales, weights, weight_scales, rounded, on_vector, pre, turned, name):
+            nc.tensor.matmul_mx(
+                out=pre[:], lhsT=tokens, lhsT_scale=token_scales, rhs=weights, rhs_scale=weight_scales,
+                start=True, stop=True,
+            )
+            positive = held(name, [P, PACK, P], F32)
+            dealt = pre[:].rearrange("s (p t) -> s t p", t=PACK)
+            if on_vector:
+                nc.vector.tensor_scalar(out=positive[:], in0=dealt, scalar1=0.0, scalar2=None, op0=ALU.max)
+            else:
+                nc.scalar.activation(out=positive[:], in_=dealt, func=ACT.Relu)
+            for t in range(PACK):
+                nc.tensor.transpose(turned[:, t * P : (t + 1) * P], positive[:, t, :], ident[:])
+            nc.scalar.activation(
+                out=rounded.rearrange("p (s t) -> p s t", t=PACK),
+                in_=turned[:].rearrange("p (t s) -> p s t", t=PACK),
+                func=ACT.Square,
+            )
+
+        h_codes, h_plane = [], []
+        for e in range(E):
+            columns = offs_sb[:, e * C // LIST_ROWS : (e + 1) * C // LIST_ROWS]
+            slot_words = held("slot_words%d" % e, [P, C], U32)
+            slot_plane = held("slot_plane%d" % e, [P, C], U8)
+            nc.vector.tensor_copy(slot_words[:], x_sb[:].bitcast(U32).indirect(columns))
+            nc.vector.tensor_copy(slot_plane[:], x_plane[:, 0, :].indirect(columns))
+            rounded = held("rounded%d" % e, [P, PASS], BF16)
+            hidden(
+                slot_words[:].bitcast(FP8X4), slot_plane[:],
+                w1_of[e].bitcast(FP4X4), w1_plane[:, e, :],
+                rounded[:], e in VECTOR_RELU_EXPERTS, banks[PRE_BANKS[e]], banks[TURN_BANKS[e]], "positive%d" % e,
+            )
+            h_codes.append(held("h_codes%d" % e, [P, C], U32))
+            h_plane.append(held("h_plane%d" % e, [P, C], U8))
+            nc.vector.quantize_mx(out=h_codes[e][:].bitcast(FP8X4), scales=h_plane[e][:], in_=rounded[:])
+
+        y_sb = [held("y_sb%d" % b, [P, SLOTS], F32) for b in range(ROW_BLOCKS)]
+        picked = [held("picked%d" % r, [P, ROW_BLOCKS, T], F32) for r in range(2)]
+        for b in range(ROW_BLOCKS):
+            for half in range(E // 4):
+                sums = banks[Y_BANKS[2 * b + half]]
+                for i in range(4):
+                    e = 4 * half + i
+                    nc.tensor.matmul_mx(
+                        out=sums[:, i * C : (i + 1) * C],
+                        lhsT=w2_sb[half][:, i, 2 * b * P : 2 * (b + 1) * P].bitcast(FP4X4),
+                        lhsT_scale=w2_plane[:, e, b * P : (b + 1) * P],
+                        rhs=h_codes[e][:].bitcast(FP8X4), rhs_scale=h_plane[e][:],
+                        start=True, stop=True,
+                    )
+                nc.scalar.copy(out=y_sb[b][:, half * PASS : (half + 1) * PASS], in_=sums[:])
+            for r in range(2):
+                nc.vector.tensor_tensor(
+                    picked[r][:, b, :], y_sb[b][:].indirect(pos_sb[r][:]), gate_sb[:, r, :], ALU.mult
+                )
+
+        out_codes = held("out_codes", [P, T], U32)
+        out_plane = held("out_plane", [P, T], U8)
+        out_rows = out_0.rearrange("(b p) t -> p b t", p=P)
+        out_words = out_1[0].rearrange("p t d -> p (t d)").bitcast(I32)
+
+        def shared(j):
+            tokens = slice(j * P, (j + 1) * P)
+            rounded = held("rounded_s%d" % j, [P, SHARED_PASSES * PASS], BF16)
+            for g in range(SHARED_PASSES):
+                unit = SHARED_PASSES * j + g
+                hidden(
+                    x_sb[:, tokens].bitcast(FP8X4), x_plane[:, 0, tokens],
+                    w1s_sb[g][:].bitcast(FP8X4), w1s_plane[:, 0, g * PASS : (g + 1) * PASS],
+                    rounded[:, g * PASS : (g + 1) * PASS], unit in VECTOR_RELU_SHARED,
+                    banks[SHARED_BANKS[unit][0]], banks[SHARED_BANKS[unit][1]], "positive_s%d" % unit,
+                )
+            codes = held("hs_codes%d" % j, [P, SHARED_PASSES * P], U32)
+            plane = held("hs_plane%d" % j, [P, SHARED_PASSES * P], U8)
+            nc.vector.quantize_mx(out=codes[:].bitcast(FP8X4), scales=plane[:], in_=rounded[:])
+            return codes, plane
+
+        def shared_out(j, codes, plane):
+            sums = banks[YS_BANKS[j]]
+            for b in range(ROW_BLOCKS):
+                for g in range(SHARED_PASSES):
+                    nc.tensor.matmul_mx(
+                        out=sums[:, b * P : (b + 1) * P],
+                        lhsT=w2s_sb[:, g, b * P : (b + 1) * P].bitcast(FP8X4),
+                        lhsT_scale=w2s_plane[:, g, b * P : (b + 1) * P],
+                        rhs=codes[:, g * P : (g + 1) * P].bitcast(FP8X4),
+                        rhs_scale=plane[:, g * P : (g + 1) * P],
+                        start=(g == 0), stop=(g == SHARED_PASSES - 1),
+                    )
+            return sums
+
+        def finish(j, sums):
+            tokens = slice(j * P, (j + 1) * P)
+            partial = held("partial%d" % j, [P, ROW_BLOCKS, P], F32)
+            nc.vector.tensor_tensor(
+                partial[:], sums[:].rearrange("p (b t) -> p b t", b=ROW_BLOCKS), picked[0][:, :, tokens], ALU.add
+            )
+            result = held("result%d" % j, [P, ROW_BLOCKS, P], F32)
+            nc.vector.tensor_tensor(result[:], partial[:], picked[1][:, :, tokens], ALU.add)
+            nc.sync.dma_start(out=out_rows[:, :, tokens], in_=result[:])
+            by_token = banks[TOKEN_BANKS[j]]
+            for b in range(ROW_BLOCKS):
+                nc.tensor.transpose(by_token[:, b * P : (b + 1) * P], result[:, b, :], ident[:])
+            pairs = held("pairs%d" % j, [P, 2, P, 2], BF16)
+            nc.scalar.copy(out=pairs[:], in_=by_token[:].rearrange("t (q u e) -> t u q e", u=2, e=2))
+            pair_words = pairs[:].rearrange("t u q e -> t (u q e)").bitcast(F32)
+            back = banks[BACK_BANKS[j]]
+            for u in range(2):
+                nc.tensor.transpose(back[:, u * P : (u + 1) * P], pair_words[:, u * P : (u + 1) * P], ident[:])
+            grouped = held("grouped%d" % j, [P, PASS], BF16)
+            nc.scalar.copy(
+                out=grouped[:].bitcast(F32).rearrange("q (t u) -> q t u", u=2),
+                in_=back[:, 0 : 2 * P].rearrange("q (u t) -> q t u", u=2),
+            )
+            nc.vector.quantize_mx(
+                out=out_codes[:, tokens].bitcast(FP8X4), scales=out_plane[:, tokens], in_=grouped[:]
+            )
+            nc.sync.dma_start(out=out_words[:, tokens], in_=out_codes[:, tokens].bitcast(I32))
+
+        hs = [shared(j) for j in range(TOKEN_TILES)]
+        for j in range(TOKEN_TILES):
+            finish(j, shared_out(j, *hs[j]))
+        for q in range(QUADS):
+            nc.sync.dma_start(
+                out=out_2[0, 4 * q : 4 * q + 4, :].bitcast(I32),
+                in_=out_plane[32 * q : 32 * q + 4, :].bitcast(I32),
+            )

@@ -26,17 +26,21 @@ ROW_BLOCKS = N // P
 TOKEN_TILES = T // P
 SHARED_PASSES = HS // PASS
 LIST_ROWS = 16
-W1_GROUPS = [1,1,2,4]
-VECTOR_RELU_EXPERTS = [4,5,6,7]
-VECTOR_RELU_SHARED = [0,1]
+W1_GROUPS = [2,2,2,2]
+VECTOR_RELU_EXPERTS = []
+VECTOR_SQUARE_EXPERTS = [7]
+VECTOR_RELU_SHARED = []
 VECTOR_SQUARE_SHARED = []
-SHARED_BANKS = [[6,7],[6,7],[0,2],[1,3],[0,2],[1,3],[0,6],[1,7]]
-YS_BANKS = [3,2,4,5]
-TOKEN_BANKS = [0,1,0,1]
-BACK_BANKS = [6,7,6,7]
-PRE_BANKS = [0,1,0,1,0,1,0,1]
-TURN_BANKS = [2,3,2,3,2,3,2,3]
+PRE_BANKS = [0,1,2,3,0,1,2,3]
 Y_BANKS = [4,5,4,5,4,5,4,5]
+SHARED_BANKS = [6,7,0,1,6,7,0,1]
+YS_BANKS = [6,0,2,3]
+TOKEN_BANKS = [4,5,4,5]
+BACK_BANKS = [7,1,7,1]
+GATHER_STARTS = {0: 2, 2: 2, 4: 2, 6: 2}
+DEAL_STARTS = {0: 2, 2: 2, 4: 2, 6: 2}
+FINISH_PIECES = [[[0,128]],[[0,128]],[[0,128]],[[0,128]]]
+RING = 2
 
 
 def tile_moe_shf_mlp_relu2_kernel(
@@ -46,6 +50,7 @@ def tile_moe_shf_mlp_relu2_kernel(
     nc = tc.nc
     with ExitStack() as ctx:
         keep = ctx.enter_context(tc.tile_pool(name="keep", bufs=1))
+        ring = ctx.enter_context(tc.tile_pool(name="ring", bufs=RING))
         psum = ctx.enter_context(tc.psum_pool(name="psum", bufs=1))
 
         def held(name, shape, dtype):
@@ -60,30 +65,21 @@ def tile_moe_shf_mlp_relu2_kernel(
                     in_=scales[:, 4 * q : 4 * q + 4, :].rearrange("g r n -> r g n").bitcast(I32),
                 )
 
-        offs_sb = keep.tile([P, SLOTS // LIST_ROWS], U16, name="offs_sb")
-        pos_sb = [keep.tile([P, T // LIST_ROWS], U16, name="pos%d_sb" % r) for r in range(2)]
-        x_sb = held("x_sb", [P, T], I32)
-        x_plane = held("x_plane", [P, 1, T], U8)
-        w1_plane = held("w1_plane", [P, E, H], U8)
-        w2_plane = held("w2_plane", [P, E, N], U8)
-        w1s_plane = held("w1s_plane", [P, 1, HS], U8)
-        w2s_plane = held("w2s_plane", [P, SHARED_PASSES, N], U8)
-        w1_sb = [held("w1_sb%d" % i, [P, n, 2 * H], U8) for i, n in enumerate(W1_GROUPS)]
-        w1_of = [w1_sb[i][:, m, :] for i, n in enumerate(W1_GROUPS) for m in range(n)]
-        w2_sb = [held("w2_sb%d" % i, [P, 4, 2 * N], U8) for i in range(E // 4)]
-        w1s_sb = [held("w1s_sb%d" % g, [P, PASS], I32) for g in range(SHARED_PASSES)]
-        w2s_sb = held("w2s_sb", [P, SHARED_PASSES, N], I32)
-        gate_sb = held("gate_sb", [P, 2, T], F32)
-        ident = held("ident", [P, P], F32)
+        def load_packed_rows(queue, plane, scales):
+            for q in range(QUADS):
+                queue.dma_start(
+                    out=plane[32 * q : 32 * q + 4 * SHARED_PASSES, :].bitcast(I32),
+                    in_=scales[:, 4 * q : 4 * q + 4, :].bitcast(I32),
+                )
 
-        nc.gpsimd.memset(x_plane[:].bitcast(I32), 0)
-        nc.vector.memset(w1_plane[:].bitcast(I32), 0)
-        make_identity(nc, ident[:])
-        nc.gpsimd.memset(w1s_plane[:].bitcast(I32), 0)
-        nc.gpsimd.memset(w2_plane[:].bitcast(I32), 0)
-        nc.gpsimd.memset(w2s_plane[:].bitcast(I32), 0)
-        warm = held("warm", [P, 1], F32)
-        nc.scalar.activation(out=warm[:], in_=ident[:, 0:1], func=ACT.Square)
+        def deal_scale_rows(queue, plane, rows, name):
+            dealt = held(name, [P, PACK, P], U8)
+            nc.vector.tensor_copy(dealt[:], rows[:].rearrange("p (m t) -> p t m", t=PACK))
+            for q in range(QUADS):
+                queue.dma_start(
+                    out=plane[32 * q : 32 * q + 4, :, :].bitcast(I32),
+                    in_=dealt[32 * q : 32 * q + 32, :, :].rearrange("p t m -> p (t m)").bitcast(I32),
+                )
 
         def load_experts(queue, tile, words, first, count):
             queue.dma_start(
@@ -91,151 +87,262 @@ def tile_moe_shf_mlp_relu2_kernel(
                 in_=words[first : first + count, 0].rearrange("e p n -> p e n").bitcast(I32),
             )
 
+        offs_sb = keep.tile([P, SLOTS // LIST_ROWS], U16, name="offs_sb")
+        pos_sb = [keep.tile([P, T // LIST_ROWS], U16, name="pos%d_sb" % r) for r in range(2)]
+        x_sb = held("x_sb", [P, T], I32)
+        x_plane = held("x_plane", [P, 1, T], U8)
+        w1_rows = held("w1_rows", [P, H], U8)
+        w2_rows = held("w2_rows", [P, N], U8)
+        w1_plane = held("w1_plane", [P, E, H], U8)
+        w2_plane = held("w2_plane", [P, E, N], U8)
+        w1s_plane = held("w1s_plane", [P, PASS], U8)
+        w2s_plane = held("w2s_plane", [P, N], U8)
+        w1_sb = [held("w1_sb%d" % i, [P, n, 2 * H], U8) for i, n in enumerate(W1_GROUPS)]
+        w1_of = [w1_sb[i][:, m, :] for i, n in enumerate(W1_GROUPS) for m in range(n)]
+        w1_in = [(lambda c, i=i, m=m: w1_sb[i][:, m : m + c, :]) for i, n in enumerate(W1_GROUPS) for m in range(n)]
+        w2_sb = [held("w2_sb%d" % i, [P, 4, 2 * N], U8) for i in range(E // 4)]
+        w1s_sb = [held("w1s_sb%d" % g, [P, PASS], I32) for g in range(SHARED_PASSES)]
+        w2s_sb = held("w2s_sb", [P, SHARED_PASSES, N], I32)
+        gate_sb = held("gate_sb", [P, 2, T], F32)
+
+        nc.gpsimd.memset(x_plane[:].bitcast(I32), 0)
+        nc.vector.memset(w1_plane[:].bitcast(I32), 0)
+        warm = held("warm", [P, 2], F32)
+        nc.gpsimd.memset(warm[:, 0:1], 0.0)
+        nc.scalar.activation(out=warm[:, 1:2], in_=warm[:, 0:1], func=ACT.Square)
+        nc.gpsimd.memset(w2_plane[:].bitcast(I32), 0)
+        nc.gpsimd.memset(w1s_plane[:].bitcast(I32), 0)
+        nc.gpsimd.memset(w2s_plane[:].bitcast(I32), 0)
+
         w1s_flat = w1s_words[0].rearrange("p l d -> p (l d)").bitcast(I32)
+        nc.sync.dma_start(out=w1_rows[:].bitcast(I32), in_=w1_scales[:, 0].rearrange("e b n -> b e n").bitcast(I32))
         nc.sync.dma_start(offs_sb[:], offs)
         load_scale_rows(nc.sync, x_plane, x_scales)
         nc.sync.dma_start(out=x_sb[:], in_=x_words[0].rearrange("p t d -> p (t d)").bitcast(I32))
-        load_experts(nc.sync, w1_sb[0], w1_words, 0, 1)
-        load_scale_rows(nc.sync, w1_plane, w1_scales[:, 0])
-        load_experts(nc.sync, w1_sb[1], w1_words, 1, 1)
-        load_experts(nc.sync, w1_sb[2], w1_words, 2, 2)
-        load_experts(nc.sync, w1_sb[3], w1_words, 4, 4)
-        load_scale_rows(nc.sync, w2_plane, w2_scales[:, 0])
+        load_experts(nc.sync, w1_sb[0], w1_words, 0, 2)
+        deal_scale_rows(nc.sync, w1_plane, w1_rows, "w1_rows_dealt")
+        load_experts(nc.sync, w1_sb[1], w1_words, 2, 2)
+        load_experts(nc.sync, w1_sb[2], w1_words, 4, 2)
+        load_experts(nc.sync, w1_sb[3], w1_words, 6, 2)
+        nc.sync.dma_start(out=w2_rows[:].bitcast(I32), in_=w2_scales[:, 0].rearrange("e b n -> b e n").bitcast(I32))
         load_experts(nc.sync, w2_sb[0], w2_words, 0, 4)
         load_experts(nc.sync, w2_sb[1], w2_words, 4, 4)
+        deal_scale_rows(nc.sync, w2_plane, w2_rows, "w2_rows_dealt")
+        load_packed_rows(nc.sync, w1s_plane, w1s_scales[0].rearrange("b (g n) -> g b n", g=SHARED_PASSES))
+        nc.sync.dma_start(out=w1s_sb[0][:], in_=w1s_flat[:, 0:PASS])
+        nc.sync.dma_start(out=w1s_sb[1][:], in_=w1s_flat[:, PASS : 2 * PASS])
         nc.sync.dma_start(pos_sb[0][:], pos1)
         nc.sync.dma_start(pos_sb[1][:], pos2)
         nc.sync.dma_start(out=gate_sb[:], in_=gate.rearrange("r p t -> p r t"))
-        load_scale_rows(nc.sync, w1s_plane, w1s_scales)
-        nc.sync.dma_start(out=w1s_sb[0][:], in_=w1s_flat[:, 0:PASS])
-        nc.sync.dma_start(out=w1s_sb[1][:], in_=w1s_flat[:, PASS : 2 * PASS])
-        load_scale_rows(nc.sync, w2s_plane, w2s_scales)
+        load_packed_rows(nc.sync, w2s_plane, w2s_scales)
         nc.sync.dma_start(out=w2s_sb[:], in_=w2s_words.rearrange("g p n d -> p g (n d)").bitcast(I32))
 
-        def hidden(tokens, token_scales, weights, weight_scales, rounded, on_vector, pre, turned, name):
-            nc.tensor.matmul_mx(
-                out=pre[:], lhsT=tokens, lhsT_scale=token_scales, rhs=weights, rhs_scale=weight_scales,
-                start=True, stop=True,
-            )
-            positive = held(name, [P, PACK, P], F32)
-            dealt = pre[:].rearrange("s (p t) -> s t p", t=PACK)
-            if on_vector:
-                nc.vector.tensor_scalar(out=positive[:], in0=dealt, scalar1=0.0, scalar2=None, op0=ALU.max)
-            else:
-                nc.scalar.activation(out=positive[:], in_=dealt, func=ACT.Relu)
+        def first_layer(weights, weight_scales, tokens, token_scales, pre, on_vector, name):
             for t in range(PACK):
-                nc.tensor.transpose(turned[:, t * P : (t + 1) * P], positive[:, t, :], ident[:])
-            nc.scalar.activation(
-                out=rounded.rearrange("p (s t) -> p s t", t=PACK),
-                in_=turned[:].rearrange("p (t s) -> p s t", t=PACK),
-                func=ACT.Square,
+                nc.tensor.matmul_mx(
+                    out=pre[:, t * P : (t + 1) * P], lhsT=weights[t], lhsT_scale=weight_scales[t],
+                    rhs=tokens, rhs_scale=token_scales, start=True, stop=True,
+                )
+            positive = held(name, [P, PASS], F32)
+            woven = pre[:].rearrange("p (t s) -> p s t", t=PACK)
+            target = positive[:].rearrange("p (s t) -> p s t", t=PACK)
+            if on_vector:
+                nc.vector.tensor_scalar(out=target, in0=woven, scalar1=0.0, scalar2=None, op0=ALU.max)
+            else:
+                nc.scalar.activation(out=target, in_=woven, func=ACT.Relu)
+            return positive
+
+        def square(rounded, positive, on_vector):
+            if on_vector:
+                nc.vector.tensor_tensor(rounded, positive[:], positive[:], ALU.mult)
+            else:
+                nc.scalar.activation(out=rounded, in_=positive[:], func=ACT.Square)
+
+        def deal_fp4(dealt, words):
+            nc.vector.tensor_copy(dealt.bitcast(U16), words.bitcast(U16).rearrange("p e (m t) -> p e t m", t=PACK))
+
+        def deal_fp8(dealt, words):
+            nc.vector.tensor_copy(
+                dealt.rearrange("p t (c i) -> p c t i", i=PACK),
+                words.rearrange("p (c i t) -> p c t i", i=PACK, t=PACK),
             )
 
         h_codes, h_plane = [], []
         for e in range(E):
-            columns = offs_sb[:, e * C // LIST_ROWS : (e + 1) * C // LIST_ROWS]
-            slot_words = held("slot_words%d" % e, [P, C], U32)
-            slot_plane = held("slot_plane%d" % e, [P, C], U8)
-            nc.vector.tensor_copy(slot_words[:], x_sb[:].bitcast(U32).indirect(columns))
-            nc.vector.tensor_copy(slot_plane[:], x_plane[:, 0, :].indirect(columns))
-            rounded = held("rounded%d" % e, [P, PASS], BF16)
-            hidden(
-                slot_words[:].bitcast(FP8X4), slot_plane[:],
-                w1_of[e].bitcast(FP4X4), w1_plane[:, e, :],
-                rounded[:], e in VECTOR_RELU_EXPERTS, banks[PRE_BANKS[e]], banks[TURN_BANKS[e]], "positive%d" % e,
+            if e in GATHER_STARTS:
+                count = GATHER_STARTS[e]
+                first = e
+                columns = offs_sb[:, e * C // LIST_ROWS : (e + count) * C // LIST_ROWS]
+                group_words = ring.tile([P, count * C], U32, name="slot_words", align_bytes=64)
+                group_plane = ring.tile([P, count * C], U8, name="slot_plane", align_bytes=64)
+                nc.vector.tensor_copy(group_words[:], x_sb[:].bitcast(U32).indirect(columns))
+                nc.vector.tensor_copy(group_plane[:], x_plane[:, 0, :].indirect(columns))
+            slot_words = group_words[:, (e - first) * C : (e - first + 1) * C]
+            slot_plane = group_plane[:, (e - first) * C : (e - first + 1) * C]
+            if e in DEAL_STARTS:
+                dfirst = e
+                group_dealt = held("w1_dealt%d" % e, [P, DEAL_STARTS[e], PACK, 2 * P], U8)
+                deal_fp4(group_dealt[:], w1_in[e](DEAL_STARTS[e]))
+            w1_dealt = group_dealt[:, e - dfirst]
+            positive = first_layer(
+                [w1_dealt[:, t, :].bitcast(FP4X4) for t in range(PACK)],
+                [w1_plane[:, e, t * P : (t + 1) * P] for t in range(PACK)],
+                slot_words.bitcast(FP8X4), slot_plane, banks[PRE_BANKS[e]],
+                e in VECTOR_RELU_EXPERTS, "positive%d" % e,
             )
+            rounded = held("rounded%d" % e, [P, PASS], BF16)
+            square(rounded[:], positive, e in VECTOR_SQUARE_EXPERTS)
             h_codes.append(held("h_codes%d" % e, [P, C], U32))
             h_plane.append(held("h_plane%d" % e, [P, C], U8))
             nc.vector.quantize_mx(out=h_codes[e][:].bitcast(FP8X4), scales=h_plane[e][:], in_=rounded[:])
 
+        w2_of = []
+        for e in range(0, E, 4):
+            w2_dealt = held("w2_dealt%d" % e, [P, 4, PACK, 2 * P], U8)
+            deal_fp4(w2_dealt[:], w2_sb[e // 4][:, e % 4 : e % 4 + 4, :])
+            w2_of.extend([w2_dealt[:, i] for i in range(4)])
+
         y_sb = [held("y_sb%d" % b, [P, SLOTS], F32) for b in range(ROW_BLOCKS)]
         picked = [held("picked%d" % r, [P, ROW_BLOCKS, T], F32) for r in range(2)]
-        for b in range(ROW_BLOCKS):
-            for half in range(E // 4):
-                sums = banks[Y_BANKS[2 * b + half]]
-                for i in range(4):
-                    e = 4 * half + i
-                    nc.tensor.matmul_mx(
-                        out=sums[:, i * C : (i + 1) * C],
-                        lhsT=w2_sb[half][:, i, 2 * b * P : 2 * (b + 1) * P].bitcast(FP4X4),
-                        lhsT_scale=w2_plane[:, e, b * P : (b + 1) * P],
-                        rhs=h_codes[e][:].bitcast(FP8X4), rhs_scale=h_plane[e][:],
-                        start=True, stop=True,
-                    )
-                nc.scalar.copy(out=y_sb[b][:, half * PASS : (half + 1) * PASS], in_=sums[:])
+
+        def slot_results(b, half):
+            sums = banks[Y_BANKS[2 * b + half]]
+            for i in range(4):
+                e = 4 * half + i
+                nc.tensor.matmul_mx(
+                    out=sums[:, i * C : (i + 1) * C],
+                    lhsT=w2_of[e][:, b, :].bitcast(FP4X4),
+                    lhsT_scale=w2_plane[:, e, b * P : (b + 1) * P],
+                    rhs=h_codes[e][:].bitcast(FP8X4), rhs_scale=h_plane[e][:],
+                    start=True, stop=True,
+                )
+            nc.scalar.copy(out=y_sb[b][:, half * PASS : (half + 1) * PASS], in_=sums[:])
+
+        def pick(b):
             for r in range(2):
                 nc.vector.tensor_tensor(
                     picked[r][:, b, :], y_sb[b][:].indirect(pos_sb[r][:]), gate_sb[:, r, :], ALU.mult
                 )
 
+        w1s_plane_dealt = held("w1s_plane_dealt", [P, PACK, P], U8)
+        w1s_dealt = [held("w1s_dealt%d" % g, [P, PACK, P], I32) for g in range(SHARED_PASSES)]
+
+        def deal_shared_1():
+            nc.vector.tensor_copy(w1s_plane_dealt[:], w1s_plane[:].rearrange("p (m t) -> p t m", t=PACK))
+            for g in range(SHARED_PASSES):
+                deal_fp8(w1s_dealt[g][:], w1s_sb[g][:])
+
+        w2s_scale_of = held("w2s_plane_dealt", [P, PACK, P], U8)
+        w2s_of = [held("w2s_dealt%d" % g, [P, PACK, P], I32) for g in range(SHARED_PASSES)]
+
+        def deal_shared_2():
+            nc.vector.tensor_copy(w2s_scale_of[:], w2s_plane[:].rearrange("p (m t) -> p t m", t=PACK))
+            for g in range(SHARED_PASSES):
+                deal_fp8(w2s_of[g][:], w2s_sb[:, g, :])
+
         out_codes = held("out_codes", [P, T], U32)
         out_plane = held("out_plane", [P, T], U8)
-        out_rows = out_0.rearrange("(b p) t -> p b t", p=P)
+        out_rows = out_0.rearrange("(p b) t -> p b t", p=P)
         out_words = out_1[0].rearrange("p t d -> p (t d)").bitcast(I32)
+        rounded_s = [held("rounded_s%d" % j, [P, SHARED_PASSES * PASS], BF16) for j in range(TOKEN_TILES)]
+        hs_codes = [held("hs_codes%d" % j, [P, SHARED_PASSES * P], U32) for j in range(TOKEN_TILES)]
+        hs_plane = [held("hs_plane%d" % j, [P, SHARED_PASSES * P], U8) for j in range(TOKEN_TILES)]
+        positive_s = {}
 
-        def shared(j):
+        def shared_relu(unit):
+            j, g = divmod(unit, SHARED_PASSES)
             tokens = slice(j * P, (j + 1) * P)
-            rounded = held("rounded_s%d" % j, [P, SHARED_PASSES * PASS], BF16)
-            for g in range(SHARED_PASSES):
-                unit = SHARED_PASSES * j + g
-                hidden(
-                    x_sb[:, tokens].bitcast(FP8X4), x_plane[:, 0, tokens],
-                    w1s_sb[g][:].bitcast(FP8X4), w1s_plane[:, 0, g * PASS : (g + 1) * PASS],
-                    rounded[:, g * PASS : (g + 1) * PASS], unit in VECTOR_RELU_SHARED,
-                    banks[SHARED_BANKS[unit][0]], banks[SHARED_BANKS[unit][1]], "positive_s%d" % unit,
-                )
-            codes = held("hs_codes%d" % j, [P, SHARED_PASSES * P], U32)
-            plane = held("hs_plane%d" % j, [P, SHARED_PASSES * P], U8)
-            nc.vector.quantize_mx(out=codes[:].bitcast(FP8X4), scales=plane[:], in_=rounded[:])
-            return codes, plane
+            positive_s.setdefault(unit, first_layer(
+                [w1s_dealt[g][:, t, :].bitcast(FP8X4) for t in range(PACK)],
+                [w1s_plane_dealt[4 * g :, t, :] for t in range(PACK)],
+                x_sb[:, tokens].bitcast(FP8X4), x_plane[:, 0, tokens], banks[SHARED_BANKS[unit]],
+                unit in VECTOR_RELU_SHARED, "positive_s%d" % unit,
+            ))
 
-        def shared_out(j, codes, plane):
+        def shared_square(unit):
+            j, g = divmod(unit, SHARED_PASSES)
+            square(rounded_s[j][:, g * PASS : (g + 1) * PASS], positive_s[unit], unit in VECTOR_SQUARE_SHARED)
+
+        def shared_quantize(j):
+            nc.vector.quantize_mx(out=hs_codes[j][:].bitcast(FP8X4), scales=hs_plane[j][:], in_=rounded_s[j][:])
+
+        def shared_out(j):
             sums = banks[YS_BANKS[j]]
             for b in range(ROW_BLOCKS):
                 for g in range(SHARED_PASSES):
                     nc.tensor.matmul_mx(
                         out=sums[:, b * P : (b + 1) * P],
-                        lhsT=w2s_sb[:, g, b * P : (b + 1) * P].bitcast(FP8X4),
-                        lhsT_scale=w2s_plane[:, g, b * P : (b + 1) * P],
-                        rhs=codes[:, g * P : (g + 1) * P].bitcast(FP8X4),
-                        rhs_scale=plane[:, g * P : (g + 1) * P],
+                        lhsT=w2s_of[g][:, b, :].bitcast(FP8X4),
+                        lhsT_scale=w2s_scale_of[4 * g :, b, :],
+                        rhs=hs_codes[j][:, g * P : (g + 1) * P].bitcast(FP8X4),
+                        rhs_scale=hs_plane[j][:, g * P : (g + 1) * P],
                         start=(g == 0), stop=(g == SHARED_PASSES - 1),
                     )
-            return sums
 
-        def finish(j, sums):
-            tokens = slice(j * P, (j + 1) * P)
-            partial = held("partial%d" % j, [P, ROW_BLOCKS, P], F32)
-            nc.vector.tensor_tensor(
-                partial[:], sums[:].rearrange("p (b t) -> p b t", b=ROW_BLOCKS), picked[0][:, :, tokens], ALU.add
-            )
-            result = held("result%d" % j, [P, ROW_BLOCKS, P], F32)
-            nc.vector.tensor_tensor(result[:], partial[:], picked[1][:, :, tokens], ALU.add)
-            nc.sync.dma_start(out=out_rows[:, :, tokens], in_=result[:])
-            by_token = banks[TOKEN_BANKS[j]]
-            for b in range(ROW_BLOCKS):
-                nc.tensor.transpose(by_token[:, b * P : (b + 1) * P], result[:, b, :], ident[:])
-            pairs = held("pairs%d" % j, [P, 2, P, 2], BF16)
-            nc.scalar.copy(out=pairs[:], in_=by_token[:].rearrange("t (q u e) -> t u q e", u=2, e=2))
-            pair_words = pairs[:].rearrange("t u q e -> t (u q e)").bitcast(F32)
-            back = banks[BACK_BANKS[j]]
-            for u in range(2):
-                nc.tensor.transpose(back[:, u * P : (u + 1) * P], pair_words[:, u * P : (u + 1) * P], ident[:])
-            grouped = held("grouped%d" % j, [P, PASS], BF16)
-            nc.scalar.copy(
-                out=grouped[:].bitcast(F32).rearrange("q (t u) -> q t u", u=2),
-                in_=back[:, 0 : 2 * P].rearrange("q (u t) -> q t u", u=2),
-            )
-            nc.vector.quantize_mx(
-                out=out_codes[:, tokens].bitcast(FP8X4), scales=out_plane[:, tokens], in_=grouped[:]
-            )
-            nc.sync.dma_start(out=out_words[:, tokens], in_=out_codes[:, tokens].bitcast(I32))
+        def finish(j):
+            for first, width in FINISH_PIECES[j]:
+                sums = banks[YS_BANKS[j]][:].rearrange("p (b t) -> p b t", b=ROW_BLOCKS)[:, :, first : first + width]
+                tokens = slice(j * P + first, j * P + first + width)
+                name = "%d_%d" % (j, first)
+                partial = held("partial" + name, [P, ROW_BLOCKS, width], F32)
+                nc.vector.tensor_tensor(partial[:], sums, picked[0][:, :, tokens], ALU.add)
+                result = held("result" + name, [P, ROW_BLOCKS, width], F32)
+                nc.vector.tensor_tensor(result[:], partial[:], picked[1][:, :, tokens], ALU.add)
+                nc.sync.dma_start(out=out_rows[:, :, tokens], in_=result[:])
+                grouped = held("grouped" + name, [P, PACK * width], BF16)
+                nc.scalar.copy(
+                    out=grouped[:].rearrange("p (c i b) -> p c b i", i=PACK, b=PACK),
+                    in_=result[:].rearrange("p b (c i) -> p c b i", i=PACK),
+                )
+                nc.vector.quantize_mx(
+                    out=out_codes[:, tokens].bitcast(FP8X4), scales=out_plane[:, tokens], in_=grouped[:]
+                )
+                nc.sync.dma_start(out=out_words[:, tokens], in_=out_codes[:, tokens].bitcast(I32))
 
-        hs = [shared(j) for j in range(TOKEN_TILES)]
-        for j in range(TOKEN_TILES):
-            finish(j, shared_out(j, *hs[j]))
+        slot_results(0, 0)
+        slot_results(0, 1)
+        pick(0)
+        deal_shared_1()
+        slot_results(1, 0)
+        slot_results(1, 1)
+        pick(1)
+        slot_results(2, 0)
+        slot_results(2, 1)
+        pick(2)
+        slot_results(3, 0)
+        slot_results(3, 1)
+        pick(3)
+        shared_relu(0)
+        shared_relu(1)
+        shared_square(0)
+        shared_square(1)
+        shared_quantize(0)
+        deal_shared_2()
+        shared_relu(2)
+        shared_relu(3)
+        shared_square(2)
+        shared_square(3)
+        shared_quantize(1)
+        shared_relu(4)
+        shared_relu(5)
+        shared_square(4)
+        shared_square(5)
+        shared_quantize(2)
+        shared_relu(6)
+        shared_relu(7)
+        shared_square(6)
+        shared_square(7)
+        shared_quantize(3)
+        shared_out(0)
+        finish(0)
+        shared_out(1)
+        finish(1)
+        shared_out(2)
+        finish(2)
+        shared_out(3)
+        finish(3)
         for q in range(QUADS):
-            nc.sync.dma_start(
+            (nc.sync, nc.scalar)[q % 2].dma_start(
                 out=out_2[0, 4 * q : 4 * q + 4, :].bitcast(I32),
                 in_=out_plane[32 * q : 32 * q + 4, :].bitcast(I32),
             )

@@ -32,9 +32,9 @@ VECTOR_SQUARE_EXPERTS = [7]
 VECTOR_RELU_SHARED = []
 VECTOR_SQUARE_SHARED = []
 PRE_BANKS = [0,1,2,3,0,1,2,3]
-Y_BANKS = [4,5,4,5,4,5,4,5]
-SHARED_BANKS = [6,7,0,1,6,7,0,1]
-YS_BANKS = [6,0,2,3]
+Y_BANKS = [4,5,6,7,6,7,6,7]
+SHARED_BANKS = [4,5,4,5,4,5,6,7]
+YS_BANKS = [4,5,6,7]
 TOKEN_BANKS = [4,5,4,5]
 BACK_BANKS = [7,1,7,1]
 GATHER_STARTS = {0: 2, 2: 2, 4: 2, 6: 2}
@@ -65,20 +65,27 @@ def tile_moe_shf_mlp_relu2_kernel(
                     in_=scales[:, 4 * q : 4 * q + 4, :].rearrange("g r n -> r g n").bitcast(I32),
                 )
 
-        def load_packed_rows(queue, plane, scales):
+        def load_packed_rows(queue, plane, scales, first):
             for q in range(QUADS):
                 queue.dma_start(
-                    out=plane[32 * q : 32 * q + 4 * SHARED_PASSES, :].bitcast(I32),
+                    out=plane[32 * q + first : 32 * q + first + 4 * SHARED_PASSES, :].bitcast(I32),
                     in_=scales[:, 4 * q : 4 * q + 4, :].bitcast(I32),
                 )
 
-        def deal_scale_rows(queue, plane, rows, name):
+        def deal_scale_rows(queues, plane, rows, name, by_row=False):
             dealt = held(name, [P, PACK, P], U8)
             nc.vector.tensor_copy(dealt[:], rows[:].rearrange("p (m t) -> p t m", t=PACK))
             for q in range(QUADS):
-                queue.dma_start(
-                    out=plane[32 * q : 32 * q + 4, :, :].bitcast(I32),
+                queues[q // 2].dma_start(
+                    out=(plane[q : P : 32, :, :] if by_row else plane[32 * q : 32 * q + 4, :, :]).bitcast(I32),
                     in_=dealt[32 * q : 32 * q + 32, :, :].rearrange("p t m -> p (t m)").bitcast(I32),
+                )
+
+        def load_expert_rows(rows, scales):
+            for r in range(4):
+                nc.sync.dma_start(
+                    out=rows[32 * r : 32 * r + 32, :].bitcast(I32),
+                    in_=scales[:, 0, r : 16 : 4, :].rearrange("e q n -> q e n").bitcast(I32),
                 )
 
         def load_experts(queue, tile, words, first, count):
@@ -96,7 +103,6 @@ def tile_moe_shf_mlp_relu2_kernel(
         w1_plane = held("w1_plane", [P, E, H], U8)
         w2_plane = held("w2_plane", [P, E, N], U8)
         w1s_plane = held("w1s_plane", [P, PASS], U8)
-        w2s_plane = held("w2s_plane", [P, N], U8)
         w1_sb = [held("w1_sb%d" % i, [P, n, 2 * H], U8) for i, n in enumerate(W1_GROUPS)]
         w1_of = [w1_sb[i][:, m, :] for i, n in enumerate(W1_GROUPS) for m in range(n)]
         w1_in = [(lambda c, i=i, m=m: w1_sb[i][:, m : m + c, :]) for i, n in enumerate(W1_GROUPS) for m in range(n)]
@@ -112,30 +118,29 @@ def tile_moe_shf_mlp_relu2_kernel(
         nc.scalar.activation(out=warm[:, 1:2], in_=warm[:, 0:1], func=ACT.Square)
         nc.gpsimd.memset(w2_plane[:].bitcast(I32), 0)
         nc.gpsimd.memset(w1s_plane[:].bitcast(I32), 0)
-        nc.gpsimd.memset(w2s_plane[:].bitcast(I32), 0)
 
         w1s_flat = w1s_words[0].rearrange("p l d -> p (l d)").bitcast(I32)
-        nc.sync.dma_start(out=w1_rows[:].bitcast(I32), in_=w1_scales[:, 0].rearrange("e b n -> b e n").bitcast(I32))
-        nc.sync.dma_start(offs_sb[:], offs)
-        load_scale_rows(nc.sync, x_plane, x_scales)
+        load_expert_rows(w1_rows, w1_scales)
         nc.sync.dma_start(out=x_sb[:], in_=x_words[0].rearrange("p t d -> p (t d)").bitcast(I32))
+        nc.sync.dma_start(offs_sb[:], offs)
         load_experts(nc.sync, w1_sb[0], w1_words, 0, 2)
-        deal_scale_rows(nc.sync, w1_plane, w1_rows, "w1_rows_dealt")
+        load_scale_rows(nc.sync, x_plane, x_scales)
+        deal_scale_rows((nc.sync, nc.sync), w1_plane, w1_rows, "w1_rows_dealt", True)
         load_experts(nc.sync, w1_sb[1], w1_words, 2, 2)
         load_experts(nc.sync, w1_sb[2], w1_words, 4, 2)
         load_experts(nc.sync, w1_sb[3], w1_words, 6, 2)
-        nc.sync.dma_start(out=w2_rows[:].bitcast(I32), in_=w2_scales[:, 0].rearrange("e b n -> b e n").bitcast(I32))
+        load_expert_rows(w2_rows, w2_scales)
         load_experts(nc.sync, w2_sb[0], w2_words, 0, 4)
         load_experts(nc.sync, w2_sb[1], w2_words, 4, 4)
-        deal_scale_rows(nc.sync, w2_plane, w2_rows, "w2_rows_dealt")
-        load_packed_rows(nc.sync, w1s_plane, w1s_scales[0].rearrange("b (g n) -> g b n", g=SHARED_PASSES))
+        load_packed_rows(nc.sync, w1s_plane, w1s_scales[0].rearrange("b (g n) -> g b n", g=SHARED_PASSES), 0)
         nc.sync.dma_start(out=w1s_sb[0][:], in_=w1s_flat[:, 0:PASS])
         nc.sync.dma_start(out=w1s_sb[1][:], in_=w1s_flat[:, PASS : 2 * PASS])
         nc.sync.dma_start(pos_sb[0][:], pos1)
         nc.sync.dma_start(pos_sb[1][:], pos2)
-        nc.sync.dma_start(out=gate_sb[:], in_=gate.rearrange("r p t -> p r t"))
-        load_packed_rows(nc.sync, w2s_plane, w2s_scales)
+        load_packed_rows(nc.sync, w1s_plane, w2s_scales, 4 * SHARED_PASSES)
+        deal_scale_rows((nc.sync, nc.sync), w2_plane, w2_rows, "w2_rows_dealt", True)
         nc.sync.dma_start(out=w2s_sb[:], in_=w2s_words.rearrange("g p n d -> p g (n d)").bitcast(I32))
+        nc.sync.dma_start(out=gate_sb[:], in_=gate.rearrange("r p t -> p r t"))
 
         def first_layer(weights, weight_scales, tokens, token_scales, pre, on_vector, name):
             for t in range(PACK):
@@ -232,11 +237,9 @@ def tile_moe_shf_mlp_relu2_kernel(
             for g in range(SHARED_PASSES):
                 deal_fp8(w1s_dealt[g][:], w1s_sb[g][:])
 
-        w2s_scale_of = held("w2s_plane_dealt", [P, PACK, P], U8)
         w2s_of = [held("w2s_dealt%d" % g, [P, PACK, P], I32) for g in range(SHARED_PASSES)]
 
         def deal_shared_2():
-            nc.vector.tensor_copy(w2s_scale_of[:], w2s_plane[:].rearrange("p (m t) -> p t m", t=PACK))
             for g in range(SHARED_PASSES):
                 deal_fp8(w2s_of[g][:], w2s_sb[:, g, :])
 
@@ -273,7 +276,7 @@ def tile_moe_shf_mlp_relu2_kernel(
                     nc.tensor.matmul_mx(
                         out=sums[:, b * P : (b + 1) * P],
                         lhsT=w2s_of[g][:, b, :].bitcast(FP8X4),
-                        lhsT_scale=w2s_scale_of[4 * g :, b, :],
+                        lhsT_scale=w1s_plane_dealt[4 * (SHARED_PASSES + g) :, b, :],
                         rhs=hs_codes[j][:, g * P : (g + 1) * P].bitcast(FP8X4),
                         rhs_scale=hs_plane[j][:, g * P : (g + 1) * P],
                         start=(g == 0), stop=(g == SHARED_PASSES - 1),
@@ -299,30 +302,30 @@ def tile_moe_shf_mlp_relu2_kernel(
                 )
                 nc.sync.dma_start(out=out_words[:, tokens], in_=out_codes[:, tokens].bitcast(I32))
 
+        deal_shared_1()
+        deal_shared_2()
         slot_results(0, 0)
         slot_results(0, 1)
         pick(0)
-        deal_shared_1()
         slot_results(1, 0)
         slot_results(1, 1)
         pick(1)
-        slot_results(2, 0)
-        slot_results(2, 1)
-        pick(2)
-        slot_results(3, 0)
-        slot_results(3, 1)
-        pick(3)
         shared_relu(0)
         shared_relu(1)
         shared_square(0)
         shared_square(1)
         shared_quantize(0)
-        deal_shared_2()
+        slot_results(2, 0)
+        slot_results(2, 1)
+        pick(2)
         shared_relu(2)
         shared_relu(3)
         shared_square(2)
         shared_square(3)
         shared_quantize(1)
+        slot_results(3, 0)
+        slot_results(3, 1)
+        pick(3)
         shared_relu(4)
         shared_relu(5)
         shared_square(4)

@@ -26,21 +26,15 @@ ROW_BLOCKS = N // P
 TOKEN_TILES = T // P
 SHARED_PASSES = HS // PASS
 LIST_ROWS = 16
-W1_GROUPS = [2,2,2,2]
-VECTOR_RELU_EXPERTS = []
-VECTOR_SQUARE_EXPERTS = [7]
-VECTOR_RELU_SHARED = []
-VECTOR_SQUARE_SHARED = []
-PRE_BANKS = [0,1,2,3,0,1,2,3]
-Y_BANKS = [4,5,6,7,6,7,6,7]
-SHARED_BANKS = [4,5,4,5,4,5,6,7]
-YS_BANKS = [4,5,6,7]
-TOKEN_BANKS = [4,5,4,5]
-BACK_BANKS = [7,1,7,1]
-GATHER_STARTS = {0: 2, 2: 2, 4: 2, 6: 2}
-DEAL_STARTS = {0: 2, 2: 2, 4: 2, 6: 2}
-FINISH_PIECES = [[[0,128]],[[0,128]],[[0,128]],[[0,128]]]
-RING = 2
+GATHER_SIZES = [1, 1, 2, 2, 2]
+VECTOR_RELU_EXPERTS = [2, 3, 4, 5, 6, 7]
+VECTOR_RELU_SHARED = [0, 1]
+Y_BANKS = [[0, 2], [1, 3], [0, 1], [6, 7]]
+SHARED_BANKS = [[4, 5], [0, 1], [2, 3], [0, 1]]
+SHARED_TURN_BANKS = [[2, 3], [4, 5], [6, 7], [2, 3]]
+YS_BANKS = [0, 1, 2, 3]
+TURN_BANKS = [4, 5, 6, 7]
+WORD_BANKS = [0, 1, 2, 3]
 
 
 def tile_moe_shf_mlp_relu2_kernel(
@@ -50,7 +44,6 @@ def tile_moe_shf_mlp_relu2_kernel(
     nc = tc.nc
     with ExitStack() as ctx:
         keep = ctx.enter_context(tc.tile_pool(name="keep", bufs=1))
-        ring = ctx.enter_context(tc.tile_pool(name="ring", bufs=RING))
         psum = ctx.enter_context(tc.psum_pool(name="psum", bufs=1))
 
         def held(name, shape, dtype):
@@ -58,34 +51,18 @@ def tile_moe_shf_mlp_relu2_kernel(
 
         banks = [psum.tile([P, PASS], F32, name="bank%d" % i) for i in range(8)]
 
-        def load_scale_rows(queue, plane, scales):
-            for q in range(QUADS):
-                queue.dma_start(
-                    out=plane[32 * q : 32 * q + 4, :, :].bitcast(I32),
-                    in_=scales[:, 4 * q : 4 * q + 4, :].rearrange("g r n -> r g n").bitcast(I32),
-                )
-
-        def load_packed_rows(queue, plane, scales, first):
-            for q in range(QUADS):
-                queue.dma_start(
-                    out=plane[32 * q + first : 32 * q + first + 4 * SHARED_PASSES, :].bitcast(I32),
-                    in_=scales[:, 4 * q : 4 * q + 4, :].bitcast(I32),
-                )
-
-        def deal_scale_rows(queues, plane, rows, name, by_row=False):
-            dealt = held(name, [P, PACK, P], U8)
-            nc.vector.tensor_copy(dealt[:], rows[:].rearrange("p (m t) -> p t m", t=PACK))
-            for q in range(QUADS):
-                queues[q // 2].dma_start(
-                    out=(plane[q : P : 32, :, :] if by_row else plane[32 * q : 32 * q + 4, :, :]).bitcast(I32),
-                    in_=dealt[32 * q : 32 * q + 32, :, :].rearrange("p t m -> p (t m)").bitcast(I32),
-                )
-
-        def load_expert_rows(rows, scales):
+        def load_rows(queues, plane, scales):
             for r in range(4):
-                nc.sync.dma_start(
-                    out=rows[32 * r : 32 * r + 32, :].bitcast(I32),
-                    in_=scales[:, 0, r : 16 : 4, :].rearrange("e q n -> q e n").bitcast(I32),
+                queues[r].dma_start(
+                    out=plane[r:P:32, :, :].bitcast(I32),
+                    in_=scales[:, r:16:4, :].rearrange("g q n -> q g n").bitcast(I32),
+                )
+
+        def load_packed_rows(queues, plane, scales):
+            for q in range(QUADS):
+                queues[q].dma_start(
+                    out=plane[32 * q : 32 * q + 4 * SHARED_PASSES, :].bitcast(I32),
+                    in_=scales[:, 4 * q : 4 * q + 4, :].bitcast(I32),
                 )
 
         def load_experts(queue, tile, words, first, count):
@@ -98,125 +75,117 @@ def tile_moe_shf_mlp_relu2_kernel(
         pos_sb = [keep.tile([P, T // LIST_ROWS], U16, name="pos%d_sb" % r) for r in range(2)]
         x_sb = held("x_sb", [P, T], I32)
         x_plane = held("x_plane", [P, 1, T], U8)
-        w1_rows = held("w1_rows", [P, H], U8)
-        w2_rows = held("w2_rows", [P, N], U8)
         w1_plane = held("w1_plane", [P, E, H], U8)
         w2_plane = held("w2_plane", [P, E, N], U8)
         w1s_plane = held("w1s_plane", [P, PASS], U8)
-        w1_sb = [held("w1_sb%d" % i, [P, n, 2 * H], U8) for i, n in enumerate(W1_GROUPS)]
-        w1_of = [w1_sb[i][:, m, :] for i, n in enumerate(W1_GROUPS) for m in range(n)]
-        w1_in = [(lambda c, i=i, m=m: w1_sb[i][:, m : m + c, :]) for i, n in enumerate(W1_GROUPS) for m in range(n)]
-        w2_sb = [held("w2_sb%d" % i, [P, 4, 2 * N], U8) for i in range(E // 4)]
+        w2s_plane = held("w2s_plane", [P, N], U8)
+        w1_sb = [held("w1_sb%d" % i, [P, 2, 2 * H], U8) for i in range(E // 2)]
+        w2_sb = held("w2_sb", [P, E, 2 * N], U8)
         w1s_sb = [held("w1s_sb%d" % g, [P, PASS], I32) for g in range(SHARED_PASSES)]
         w2s_sb = held("w2s_sb", [P, SHARED_PASSES, N], I32)
         gate_sb = held("gate_sb", [P, 2, T], F32)
+        identity = held("identity", [P, P], F32)
 
         nc.gpsimd.memset(x_plane[:].bitcast(I32), 0)
-        nc.vector.memset(w1_plane[:].bitcast(I32), 0)
-        warm = held("warm", [P, 2], F32)
-        nc.gpsimd.memset(warm[:, 0:1], 0.0)
-        nc.scalar.activation(out=warm[:, 1:2], in_=warm[:, 0:1], func=ACT.Square)
-        nc.gpsimd.memset(w2_plane[:].bitcast(I32), 0)
-        nc.gpsimd.memset(w1s_plane[:].bitcast(I32), 0)
+        nc.gpsimd.memset(w1_plane[:, 0 : E // 2, :].bitcast(I32), 0)
+        nc.vector.memset(w1_plane[:, E // 2 : E, :].bitcast(I32), 0)
+        nc.vector.memset(w1s_plane[:].bitcast(I32), 0)
+        nc.vector.memset(w2_plane[:].bitcast(I32), 0)
+        make_identity(nc, identity[:])
+        nc.gpsimd.memset(w2s_plane[:].bitcast(I32), 0)
 
+        sync4 = (nc.sync,) * 4
+        both = (nc.sync, nc.scalar, nc.sync, nc.scalar)
         w1s_flat = w1s_words[0].rearrange("p l d -> p (l d)").bitcast(I32)
-        load_expert_rows(w1_rows, w1_scales)
         nc.sync.dma_start(out=x_sb[:], in_=x_words[0].rearrange("p t d -> p (t d)").bitcast(I32))
+        load_rows(both, x_plane, x_scales)
         nc.sync.dma_start(offs_sb[:], offs)
         load_experts(nc.sync, w1_sb[0], w1_words, 0, 2)
-        load_scale_rows(nc.sync, x_plane, x_scales)
-        deal_scale_rows((nc.sync, nc.sync), w1_plane, w1_rows, "w1_rows_dealt", True)
+        load_rows((nc.scalar, nc.scalar, nc.sync, nc.sync), w1_plane, w1_scales[:, 0])
         load_experts(nc.sync, w1_sb[1], w1_words, 2, 2)
         load_experts(nc.sync, w1_sb[2], w1_words, 4, 2)
         load_experts(nc.sync, w1_sb[3], w1_words, 6, 2)
-        load_expert_rows(w2_rows, w2_scales)
-        load_experts(nc.sync, w2_sb[0], w2_words, 0, 4)
-        load_experts(nc.sync, w2_sb[1], w2_words, 4, 4)
-        load_packed_rows(nc.sync, w1s_plane, w1s_scales[0].rearrange("b (g n) -> g b n", g=SHARED_PASSES), 0)
+        load_packed_rows(sync4, w1s_plane, w1s_scales[0].rearrange("b (g n) -> g b n", g=SHARED_PASSES))
         nc.sync.dma_start(out=w1s_sb[0][:], in_=w1s_flat[:, 0:PASS])
         nc.sync.dma_start(out=w1s_sb[1][:], in_=w1s_flat[:, PASS : 2 * PASS])
+        load_rows(sync4, w2_plane, w2_scales[:, 0])
+        load_experts(nc.sync, w2_sb, w2_words, 0, E)
         nc.sync.dma_start(pos_sb[0][:], pos1)
         nc.sync.dma_start(pos_sb[1][:], pos2)
-        load_packed_rows(nc.sync, w1s_plane, w2s_scales, 4 * SHARED_PASSES)
-        deal_scale_rows((nc.sync, nc.sync), w2_plane, w2_rows, "w2_rows_dealt", True)
-        nc.sync.dma_start(out=w2s_sb[:], in_=w2s_words.rearrange("g p n d -> p g (n d)").bitcast(I32))
         nc.sync.dma_start(out=gate_sb[:], in_=gate.rearrange("r p t -> p r t"))
+        load_packed_rows(sync4, w2s_plane, w2s_scales)
+        nc.sync.dma_start(out=w2s_sb[:], in_=w2s_words.rearrange("g p n d -> p g (n d)").bitcast(I32))
 
-        def first_layer(weights, weight_scales, tokens, token_scales, pre, on_vector, name):
-            for t in range(PACK):
-                nc.tensor.matmul_mx(
-                    out=pre[:, t * P : (t + 1) * P], lhsT=weights[t], lhsT_scale=weight_scales[t],
-                    rhs=tokens, rhs_scale=token_scales, start=True, stop=True,
-                )
+        def product(tokens, token_scales, weights, weight_scales, pre):
+            nc.tensor.matmul_mx(
+                out=pre[:], lhsT=tokens, lhsT_scale=token_scales, rhs=weights, rhs_scale=weight_scales,
+                start=True, stop=True,
+            )
+
+        def relu(pre, on_vector, name):
             positive = held(name, [P, PASS], F32)
-            woven = pre[:].rearrange("p (t s) -> p s t", t=PACK)
-            target = positive[:].rearrange("p (s t) -> p s t", t=PACK)
+            dealt = pre[:].rearrange("p (m t) -> p t m", t=PACK)
+            target = positive[:].rearrange("p (t m) -> p t m", t=PACK)
             if on_vector:
-                nc.vector.tensor_scalar(out=target, in0=woven, scalar1=0.0, scalar2=None, op0=ALU.max)
+                nc.vector.tensor_scalar(out=target, in0=dealt, scalar1=0.0, scalar2=None, op0=ALU.max)
             else:
-                nc.scalar.activation(out=target, in_=woven, func=ACT.Relu)
+                nc.scalar.activation(out=target, in_=dealt, func=ACT.Relu)
             return positive
 
-        def square(rounded, positive, on_vector):
-            if on_vector:
-                nc.vector.tensor_tensor(rounded, positive[:], positive[:], ALU.mult)
-            else:
-                nc.scalar.activation(out=rounded, in_=positive[:], func=ACT.Square)
+        def turn(turned, source, count):
+            for t in range(count):
+                nc.tensor.transpose(turned[:, t * P : (t + 1) * P], source[:, t * P : (t + 1) * P], identity[:])
 
-        def deal_fp4(dealt, words):
-            nc.vector.tensor_copy(dealt.bitcast(U16), words.bitcast(U16).rearrange("p e (m t) -> p e t m", t=PACK))
-
-        def deal_fp8(dealt, words):
-            nc.vector.tensor_copy(
-                dealt.rearrange("p t (c i) -> p c t i", i=PACK),
-                words.rearrange("p (c i t) -> p c t i", i=PACK, t=PACK),
+        def square(rounded, turned):
+            nc.scalar.activation(
+                out=rounded.rearrange("p (s t) -> p s t", t=PACK),
+                in_=turned[:].rearrange("p (t s) -> p s t", t=PACK), func=ACT.Square,
             )
 
-        h_codes, h_plane = [], []
-        for e in range(E):
-            if e in GATHER_STARTS:
-                count = GATHER_STARTS[e]
-                first = e
-                columns = offs_sb[:, e * C // LIST_ROWS : (e + count) * C // LIST_ROWS]
-                group_words = ring.tile([P, count * C], U32, name="slot_words", align_bytes=64)
-                group_plane = ring.tile([P, count * C], U8, name="slot_plane", align_bytes=64)
-                nc.vector.tensor_copy(group_words[:], x_sb[:].bitcast(U32).indirect(columns))
-                nc.vector.tensor_copy(group_plane[:], x_plane[:, 0, :].indirect(columns))
-            slot_words = group_words[:, (e - first) * C : (e - first + 1) * C]
-            slot_plane = group_plane[:, (e - first) * C : (e - first + 1) * C]
-            if e in DEAL_STARTS:
-                dfirst = e
-                group_dealt = held("w1_dealt%d" % e, [P, DEAL_STARTS[e], PACK, 2 * P], U8)
-                deal_fp4(group_dealt[:], w1_in[e](DEAL_STARTS[e]))
-            w1_dealt = group_dealt[:, e - dfirst]
-            positive = first_layer(
-                [w1_dealt[:, t, :].bitcast(FP4X4) for t in range(PACK)],
-                [w1_plane[:, e, t * P : (t + 1) * P] for t in range(PACK)],
-                slot_words.bitcast(FP8X4), slot_plane, banks[PRE_BANKS[e]],
-                e in VECTOR_RELU_EXPERTS, "positive%d" % e,
-            )
-            rounded = held("rounded%d" % e, [P, PASS], BF16)
-            square(rounded[:], positive, e in VECTOR_SQUARE_EXPERTS)
-            h_codes.append(held("h_codes%d" % e, [P, C], U32))
-            h_plane.append(held("h_plane%d" % e, [P, C], U8))
-            nc.vector.quantize_mx(out=h_codes[e][:].bitcast(FP8X4), scales=h_plane[e][:], in_=rounded[:])
+        slot_words, slot_plane = [], []
+        first = 0
+        for count in GATHER_SIZES:
+            columns = offs_sb[:, first * C // LIST_ROWS : (first + count) * C // LIST_ROWS]
+            words = held("slot_words%d" % first, [P, count * C], U32)
+            plane = held("slot_plane%d" % first, [P, count * C], U8)
+            slot_words.extend([(words, plane, columns, i) for i in range(count)])
+            first = first + count
 
-        w2_of = []
-        for e in range(0, E, 4):
-            w2_dealt = held("w2_dealt%d" % e, [P, 4, PACK, 2 * P], U8)
-            deal_fp4(w2_dealt[:], w2_sb[e // 4][:, e % 4 : e % 4 + 4, :])
-            w2_of.extend([w2_dealt[:, i] for i in range(4)])
+        h_codes = [held("h_codes%d" % e, [P, C], U32) for e in range(E)]
+        h_plane = [held("h_plane%d" % e, [P, C], U8) for e in range(E)]
+        rounded = [held("rounded%d" % e, [P, PASS], BF16) for e in range(E)]
+        positive = {}
+
+        def routed_product(e):
+            words, plane, columns, i = slot_words[e]
+            if i == 0:
+                nc.vector.tensor_copy(plane[:], x_plane[:, 0, :].indirect(columns))
+                nc.vector.tensor_copy(words[:], x_sb[:].bitcast(U32).indirect(columns))
+            product(
+                words[:, i * C : (i + 1) * C].bitcast(FP8X4), plane[:, i * C : (i + 1) * C],
+                w1_sb[e // 2][:, e % 2, :].bitcast(FP4X4), w1_plane[:, e, :], banks[e],
+            )
+
+        def routed_relu(e):
+            positive.setdefault(e, relu(banks[e], e in VECTOR_RELU_EXPERTS, "positive%d" % e))
+
+        def routed_square(e):
+            turn(banks[e], positive[e], PACK)
+            square(rounded[e][:], banks[e])
+
+        def routed_quantize(e):
+            nc.vector.quantize_mx(out=h_codes[e][:].bitcast(FP8X4), scales=h_plane[e][:], in_=rounded[e][:])
 
         y_sb = [held("y_sb%d" % b, [P, SLOTS], F32) for b in range(ROW_BLOCKS)]
         picked = [held("picked%d" % r, [P, ROW_BLOCKS, T], F32) for r in range(2)]
 
         def slot_results(b, half):
-            sums = banks[Y_BANKS[2 * b + half]]
+            sums = banks[Y_BANKS[b][half]]
             for i in range(4):
                 e = 4 * half + i
                 nc.tensor.matmul_mx(
                     out=sums[:, i * C : (i + 1) * C],
-                    lhsT=w2_of[e][:, b, :].bitcast(FP4X4),
+                    lhsT=w2_sb[:, e, 2 * b * P : 2 * (b + 1) * P].bitcast(FP4X4),
                     lhsT_scale=w2_plane[:, e, b * P : (b + 1) * P],
                     rhs=h_codes[e][:].bitcast(FP8X4), rhs_scale=h_plane[e][:],
                     start=True, stop=True,
@@ -229,42 +198,31 @@ def tile_moe_shf_mlp_relu2_kernel(
                     picked[r][:, b, :], y_sb[b][:].indirect(pos_sb[r][:]), gate_sb[:, r, :], ALU.mult
                 )
 
-        w1s_plane_dealt = held("w1s_plane_dealt", [P, PACK, P], U8)
-        w1s_dealt = [held("w1s_dealt%d" % g, [P, PACK, P], I32) for g in range(SHARED_PASSES)]
-
-        def deal_shared_1():
-            nc.vector.tensor_copy(w1s_plane_dealt[:], w1s_plane[:].rearrange("p (m t) -> p t m", t=PACK))
-            for g in range(SHARED_PASSES):
-                deal_fp8(w1s_dealt[g][:], w1s_sb[g][:])
-
-        w2s_of = [held("w2s_dealt%d" % g, [P, PACK, P], I32) for g in range(SHARED_PASSES)]
-
-        def deal_shared_2():
-            for g in range(SHARED_PASSES):
-                deal_fp8(w2s_of[g][:], w2s_sb[:, g, :])
-
-        out_codes = held("out_codes", [P, T], U32)
-        out_plane = held("out_plane", [P, T], U8)
-        out_rows = out_0.rearrange("(p b) t -> p b t", p=P)
-        out_words = out_1[0].rearrange("p t d -> p (t d)").bitcast(I32)
         rounded_s = [held("rounded_s%d" % j, [P, SHARED_PASSES * PASS], BF16) for j in range(TOKEN_TILES)]
         hs_codes = [held("hs_codes%d" % j, [P, SHARED_PASSES * P], U32) for j in range(TOKEN_TILES)]
         hs_plane = [held("hs_plane%d" % j, [P, SHARED_PASSES * P], U8) for j in range(TOKEN_TILES)]
-        positive_s = {}
 
-        def shared_relu(unit):
-            j, g = divmod(unit, SHARED_PASSES)
+        kept = {}
+
+        def shared_product(j):
             tokens = slice(j * P, (j + 1) * P)
-            positive_s.setdefault(unit, first_layer(
-                [w1s_dealt[g][:, t, :].bitcast(FP8X4) for t in range(PACK)],
-                [w1s_plane_dealt[4 * g :, t, :] for t in range(PACK)],
-                x_sb[:, tokens].bitcast(FP8X4), x_plane[:, 0, tokens], banks[SHARED_BANKS[unit]],
-                unit in VECTOR_RELU_SHARED, "positive_s%d" % unit,
-            ))
+            for g in range(SHARED_PASSES):
+                product(
+                    x_sb[:, tokens].bitcast(FP8X4), x_plane[:, 0, tokens],
+                    w1s_sb[g][:].bitcast(FP8X4), w1s_plane[4 * g :, :], banks[SHARED_BANKS[j][g]],
+                )
 
-        def shared_square(unit):
-            j, g = divmod(unit, SHARED_PASSES)
-            square(rounded_s[j][:, g * PASS : (g + 1) * PASS], positive_s[unit], unit in VECTOR_SQUARE_SHARED)
+        def shared_relu(j):
+            kept.setdefault(j, [
+                relu(banks[SHARED_BANKS[j][g]], SHARED_PASSES * j + g in VECTOR_RELU_SHARED, "positive_s%d_%d" % (j, g))
+                for g in range(SHARED_PASSES)
+            ])
+
+        def shared_square(j):
+            for g in range(SHARED_PASSES):
+                turn(banks[SHARED_TURN_BANKS[j][g]], kept[j][g], PACK)
+            for g in range(SHARED_PASSES):
+                square(rounded_s[j][:, g * PASS : (g + 1) * PASS], banks[SHARED_TURN_BANKS[j][g]])
 
         def shared_quantize(j):
             nc.vector.quantize_mx(out=hs_codes[j][:].bitcast(FP8X4), scales=hs_plane[j][:], in_=rounded_s[j][:])
@@ -275,75 +233,95 @@ def tile_moe_shf_mlp_relu2_kernel(
                 for g in range(SHARED_PASSES):
                     nc.tensor.matmul_mx(
                         out=sums[:, b * P : (b + 1) * P],
-                        lhsT=w2s_of[g][:, b, :].bitcast(FP8X4),
-                        lhsT_scale=w1s_plane_dealt[4 * (SHARED_PASSES + g) :, b, :],
+                        lhsT=w2s_sb[:, g, b * P : (b + 1) * P].bitcast(FP8X4),
+                        lhsT_scale=w2s_plane[4 * g :, b * P : (b + 1) * P],
                         rhs=hs_codes[j][:, g * P : (g + 1) * P].bitcast(FP8X4),
                         rhs_scale=hs_plane[j][:, g * P : (g + 1) * P],
                         start=(g == 0), stop=(g == SHARED_PASSES - 1),
                     )
 
-        def finish(j):
-            for first, width in FINISH_PIECES[j]:
-                sums = banks[YS_BANKS[j]][:].rearrange("p (b t) -> p b t", b=ROW_BLOCKS)[:, :, first : first + width]
-                tokens = slice(j * P + first, j * P + first + width)
-                name = "%d_%d" % (j, first)
-                partial = held("partial" + name, [P, ROW_BLOCKS, width], F32)
-                nc.vector.tensor_tensor(partial[:], sums, picked[0][:, :, tokens], ALU.add)
-                result = held("result" + name, [P, ROW_BLOCKS, width], F32)
-                nc.vector.tensor_tensor(result[:], partial[:], picked[1][:, :, tokens], ALU.add)
-                nc.sync.dma_start(out=out_rows[:, :, tokens], in_=result[:])
-                grouped = held("grouped" + name, [P, PACK * width], BF16)
-                nc.scalar.copy(
-                    out=grouped[:].rearrange("p (c i b) -> p c b i", i=PACK, b=PACK),
-                    in_=result[:].rearrange("p b (c i) -> p c b i", i=PACK),
-                )
-                nc.vector.quantize_mx(
-                    out=out_codes[:, tokens].bitcast(FP8X4), scales=out_plane[:, tokens], in_=grouped[:]
-                )
-                nc.sync.dma_start(out=out_words[:, tokens], in_=out_codes[:, tokens].bitcast(I32))
+        out_codes = held("out_codes", [P, T], U32)
+        out_plane = held("out_plane", [P, T], U8)
+        out_rows = out_0.rearrange("(b p) t -> p b t", p=P)
+        out_words = out_1[0].rearrange("p t d -> p (t d)").bitcast(I32)
+        routed = [held("routed%d" % j, [P, ROW_BLOCKS, P], F32) for j in range(TOKEN_TILES)]
+        result = [held("result%d" % j, [P, ROW_BLOCKS * P], F32) for j in range(TOKEN_TILES)]
+        grouped = [held("grouped%d" % j, [P, PACK * P], BF16) for j in range(TOKEN_TILES)]
 
-        deal_shared_1()
-        deal_shared_2()
-        slot_results(0, 0)
-        slot_results(0, 1)
-        pick(0)
-        slot_results(1, 0)
-        slot_results(1, 1)
-        pick(1)
+        def add_picked(j):
+            tokens = slice(j * P, (j + 1) * P)
+            sums = banks[YS_BANKS[j]][:].rearrange("p (b t) -> p b t", b=ROW_BLOCKS)
+            nc.vector.tensor_tensor(routed[j][:], sums, picked[0][:, :, tokens], ALU.add)
+
+        def finish(j):
+            tokens = slice(j * P, (j + 1) * P)
+            nc.vector.tensor_tensor(
+                result[j][:].rearrange("p (b t) -> p b t", b=ROW_BLOCKS), routed[j][:], picked[1][:, :, tokens], ALU.add
+            )
+            nc.sync.dma_start(out=out_rows[:, :, tokens], in_=result[j][:].rearrange("p (b t) -> p b t", b=ROW_BLOCKS))
+            turn(banks[TURN_BANKS[j]], result[j], ROW_BLOCKS)
+            pairs = held("pairs%d" % j, [P, N], BF16)
+            nc.scalar.copy(
+                out=pairs[:].rearrange("p (u m e) -> p u m e", u=2, e=2),
+                in_=banks[TURN_BANKS[j]][:].rearrange("p (m u e) -> p u m e", u=2, e=2),
+            )
+            turn(banks[WORD_BANKS[j]], pairs[:].bitcast(F32), 2)
+            nc.scalar.copy(
+                out=grouped[j][:].bitcast(F32).rearrange("p (t u) -> p t u", u=2),
+                in_=banks[WORD_BANKS[j]][:, 0 : 2 * P].rearrange("p (u t) -> p t u", u=2),
+            )
+
+        def hand_on(j):
+            tokens = slice(j * P, (j + 1) * P)
+            nc.vector.quantize_mx(
+                out=out_codes[:, tokens].bitcast(FP8X4), scales=out_plane[:, tokens], in_=grouped[j][:]
+            )
+            nc.sync.dma_start(out=out_words[:, tokens], in_=out_codes[:, tokens].bitcast(I32))
+
+        for e in range(E + 4):
+            if e < E:
+                routed_product(e)
+            if e >= 3 and e % 2 == 1:
+                for done in (e - 3, e - 2):
+                    if done < E:
+                        routed_relu(done)
+                        routed_square(done)
+                        routed_quantize(done)
+        shared_product(0)
         shared_relu(0)
-        shared_relu(1)
-        shared_square(0)
-        shared_square(1)
-        shared_quantize(0)
+        slot_results(0, 0)
+        slot_results(1, 0)
+        slot_results(0, 1)
+        slot_results(1, 1)
+        pick(0)
         slot_results(2, 0)
         slot_results(2, 1)
-        pick(2)
-        shared_relu(2)
-        shared_relu(3)
-        shared_square(2)
-        shared_square(3)
-        shared_quantize(1)
+        shared_square(0)
+        pick(1)
+        shared_quantize(0)
         slot_results(3, 0)
         slot_results(3, 1)
+        shared_product(1)
+        shared_relu(1)
+        shared_square(1)
+        pick(2)
         pick(3)
-        shared_relu(4)
-        shared_relu(5)
-        shared_square(4)
-        shared_square(5)
-        shared_quantize(2)
-        shared_relu(6)
-        shared_relu(7)
-        shared_square(6)
-        shared_square(7)
-        shared_quantize(3)
-        shared_out(0)
-        finish(0)
-        shared_out(1)
-        finish(1)
-        shared_out(2)
-        finish(2)
-        shared_out(3)
-        finish(3)
+        shared_quantize(1)
+        for j in (2, 3):
+            shared_product(j)
+            shared_relu(j)
+        for j in (2, 3):
+            shared_square(j)
+            shared_quantize(j)
+        for j in range(TOKEN_TILES):
+            shared_out(j)
+        for pair in range(0, TOKEN_TILES, 2):
+            add_picked(pair)
+            add_picked(pair + 1)
+            finish(pair)
+            finish(pair + 1)
+        for j in range(TOKEN_TILES):
+            hand_on(j)
         for q in range(QUADS):
             (nc.sync, nc.scalar)[q % 2].dma_start(
                 out=out_2[0, 4 * q : 4 * q + 4, :].bitcast(I32),

@@ -27,14 +27,14 @@ TOKEN_TILES = T // P
 SHARED_PASSES = HS // PASS
 LIST_ROWS = 16
 GATHER_SIZES = [1, 1, 2, 2, 2]
-VECTOR_RELU_EXPERTS = [2, 3, 4, 5, 6, 7]
-VECTOR_RELU_SHARED = [0, 1]
-Y_BANKS = [[0, 2], [1, 3], [0, 1], [6, 7]]
-SHARED_BANKS = [[4, 5], [0, 1], [2, 3], [0, 1]]
-SHARED_TURN_BANKS = [[2, 3], [4, 5], [6, 7], [2, 3]]
-YS_BANKS = [0, 1, 2, 3]
-TURN_BANKS = [4, 5, 6, 7]
-WORD_BANKS = [0, 1, 2, 3]
+VECTOR_RELU_EXPERTS = [4, 5, 6, 7]
+VECTOR_RELU_SHARED = []
+VECTOR_ROUND = [3]
+AHEAD = 2
+Y_BANKS = [[0, 2], [1, 3], [4, 5], [6, 7]]
+SHARED_BANKS = [[0, 1], [2, 3], [4, 5], [6, 7]]
+SHARED_TURN_BANKS = [[0, 1], [2, 3], [4, 5], [6, 7]]
+YS_BANKS = [0, 4, 5, 1]
 
 
 def tile_moe_shf_mlp_relu2_kernel(
@@ -80,11 +80,18 @@ def tile_moe_shf_mlp_relu2_kernel(
         w1s_plane = held("w1s_plane", [P, PASS], U8)
         w2s_plane = held("w2s_plane", [P, N], U8)
         w1_sb = [held("w1_sb%d" % i, [P, 2, 2 * H], U8) for i in range(E // 2)]
-        w2_sb = held("w2_sb", [P, E, 2 * N], U8)
+        w2_sb = [held("w2_sb%d" % i, [P, 4, 2 * N], U8) for i in range(E // 4)]
+        w2_rows = held("w2_rows", [P, N], U8)
+        w2_rows_dealt = held("w2_rows_dealt", [P, PACK, P], U8)
         w1s_sb = [held("w1s_sb%d" % g, [P, PASS], I32) for g in range(SHARED_PASSES)]
         w2s_sb = held("w2s_sb", [P, SHARED_PASSES, N], I32)
         gate_sb = held("gate_sb", [P, 2, T], F32)
         identity = held("identity", [P, P], F32)
+        w2_dealt = [
+            [held("w2_dealt%d_%d" % (i, u), [P, 4, 2, 2 * P], U8) for u in range(2)] for i in range(E // 4)
+        ]
+        w2s_dealt = [held("w2s_dealt%d" % g, [P, PACK, P], I32) for g in range(SHARED_PASSES)]
+        w2s_plane_dealt = held("w2s_plane_dealt", [P, PACK, P], U8)
 
         nc.gpsimd.memset(x_plane[:].bitcast(I32), 0)
         nc.gpsimd.memset(w1_plane[:, 0 : E // 2, :].bitcast(I32), 0)
@@ -102,19 +109,42 @@ def tile_moe_shf_mlp_relu2_kernel(
         nc.sync.dma_start(offs_sb[:], offs)
         load_experts(nc.sync, w1_sb[0], w1_words, 0, 2)
         load_rows((nc.scalar, nc.scalar, nc.sync, nc.sync), w1_plane, w1_scales[:, 0])
+        nc.sync.dma_start(
+            out=w2_rows[:].bitcast(I32), in_=w2_scales[:, 0].rearrange("e b n -> b e n").bitcast(I32)
+        )
         load_experts(nc.sync, w1_sb[1], w1_words, 2, 2)
         load_experts(nc.sync, w1_sb[2], w1_words, 4, 2)
         load_experts(nc.sync, w1_sb[3], w1_words, 6, 2)
-        load_packed_rows(sync4, w1s_plane, w1s_scales[0].rearrange("b (g n) -> g b n", g=SHARED_PASSES))
-        nc.sync.dma_start(out=w1s_sb[0][:], in_=w1s_flat[:, 0:PASS])
-        nc.sync.dma_start(out=w1s_sb[1][:], in_=w1s_flat[:, PASS : 2 * PASS])
-        load_rows(sync4, w2_plane, w2_scales[:, 0])
-        load_experts(nc.sync, w2_sb, w2_words, 0, E)
-        nc.sync.dma_start(pos_sb[0][:], pos1)
-        nc.sync.dma_start(pos_sb[1][:], pos2)
-        nc.sync.dma_start(out=gate_sb[:], in_=gate.rearrange("r p t -> p r t"))
+        for i in range(E // 4):
+            load_experts(nc.sync, w2_sb[i], w2_words, 4 * i, 4)
         load_packed_rows(sync4, w2s_plane, w2s_scales)
         nc.sync.dma_start(out=w2s_sb[:], in_=w2s_words.rearrange("g p n d -> p g (n d)").bitcast(I32))
+
+        def load_rest():
+            for q in range(QUADS):
+                nc.sync.dma_start(
+                    out=w2_plane[32 * q : 32 * q + 4, :, :].bitcast(I32),
+                    in_=w2_rows_dealt[32 * q : 32 * q + 32, :, :].rearrange("p t m -> p (t m)").bitcast(I32),
+                )
+            load_packed_rows(sync4, w1s_plane, w1s_scales[0].rearrange("b (g n) -> g b n", g=SHARED_PASSES))
+            nc.sync.dma_start(out=w1s_sb[0][:], in_=w1s_flat[:, 0:PASS])
+            nc.sync.dma_start(out=w1s_sb[1][:], in_=w1s_flat[:, PASS : 2 * PASS])
+            nc.sync.dma_start(pos_sb[0][:], pos1)
+            nc.sync.dma_start(pos_sb[1][:], pos2)
+            nc.sync.dma_start(out=gate_sb[:], in_=gate.rearrange("r p t -> p r t"))
+
+        def deal_bytes(dealt, rows):
+            nc.vector.tensor_copy(dealt[:], rows[:].rearrange("p (m t) -> p t m", t=PACK))
+
+        def deal_fp4(i, u):
+            columns = w2_sb[i][:].bitcast(U16).rearrange("p e (m t) -> p e t m", t=PACK)
+            nc.vector.tensor_copy(w2_dealt[i][u][:].bitcast(U16), columns[:, :, 2 * u : 2 * u + 2, :])
+
+        def deal_fp8(g):
+            nc.vector.tensor_copy(
+                w2s_dealt[g][:].rearrange("p t (c i) -> p c t i", i=PACK),
+                w2s_sb[:, g, :].rearrange("p (c i t) -> p c t i", i=PACK, t=PACK),
+            )
 
         def product(tokens, token_scales, weights, weight_scales, pre):
             nc.tensor.matmul_mx(
@@ -169,8 +199,10 @@ def tile_moe_shf_mlp_relu2_kernel(
         def routed_relu(e):
             positive.setdefault(e, relu(banks[e], e in VECTOR_RELU_EXPERTS, "positive%d" % e))
 
-        def routed_square(e):
+        def routed_turn(e):
             turn(banks[e], positive[e], PACK)
+
+        def routed_square(e):
             square(rounded[e][:], banks[e])
 
         def routed_quantize(e):
@@ -185,7 +217,7 @@ def tile_moe_shf_mlp_relu2_kernel(
                 e = 4 * half + i
                 nc.tensor.matmul_mx(
                     out=sums[:, i * C : (i + 1) * C],
-                    lhsT=w2_sb[:, e, 2 * b * P : 2 * (b + 1) * P].bitcast(FP4X4),
+                    lhsT=w2_dealt[half][b // 2][:, i, b % 2, :].bitcast(FP4X4),
                     lhsT_scale=w2_plane[:, e, b * P : (b + 1) * P],
                     rhs=h_codes[e][:].bitcast(FP8X4), rhs_scale=h_plane[e][:],
                     start=True, stop=True,
@@ -233,8 +265,8 @@ def tile_moe_shf_mlp_relu2_kernel(
                 for g in range(SHARED_PASSES):
                     nc.tensor.matmul_mx(
                         out=sums[:, b * P : (b + 1) * P],
-                        lhsT=w2s_sb[:, g, b * P : (b + 1) * P].bitcast(FP8X4),
-                        lhsT_scale=w2s_plane[4 * g :, b * P : (b + 1) * P],
+                        lhsT=w2s_dealt[g][:, b, :].bitcast(FP8X4),
+                        lhsT_scale=w2s_plane_dealt[4 * g :, b, :],
                         rhs=hs_codes[j][:, g * P : (g + 1) * P].bitcast(FP8X4),
                         rhs_scale=hs_plane[j][:, g * P : (g + 1) * P],
                         start=(g == 0), stop=(g == SHARED_PASSES - 1),
@@ -242,7 +274,7 @@ def tile_moe_shf_mlp_relu2_kernel(
 
         out_codes = held("out_codes", [P, T], U32)
         out_plane = held("out_plane", [P, T], U8)
-        out_rows = out_0.rearrange("(b p) t -> p b t", p=P)
+        out_rows = out_0.rearrange("(p b) t -> p b t", p=P)
         out_words = out_1[0].rearrange("p t d -> p (t d)").bitcast(I32)
         routed = [held("routed%d" % j, [P, ROW_BLOCKS, P], F32) for j in range(TOKEN_TILES)]
         result = [held("result%d" % j, [P, ROW_BLOCKS * P], F32) for j in range(TOKEN_TILES)]
@@ -250,76 +282,75 @@ def tile_moe_shf_mlp_relu2_kernel(
 
         def add_picked(j):
             tokens = slice(j * P, (j + 1) * P)
-            sums = banks[YS_BANKS[j]][:].rearrange("p (b t) -> p b t", b=ROW_BLOCKS)
-            nc.vector.tensor_tensor(routed[j][:], sums, picked[0][:, :, tokens], ALU.add)
+            nc.vector.tensor_tensor(routed[j][:], picked[0][:, :, tokens], picked[1][:, :, tokens], ALU.add)
 
         def finish(j):
             tokens = slice(j * P, (j + 1) * P)
             nc.vector.tensor_tensor(
-                result[j][:].rearrange("p (b t) -> p b t", b=ROW_BLOCKS), routed[j][:], picked[1][:, :, tokens], ALU.add
+                result[j][:], banks[YS_BANKS[j]][:], routed[j][:].rearrange("p b t -> p (b t)"), ALU.add
             )
             nc.sync.dma_start(out=out_rows[:, :, tokens], in_=result[j][:].rearrange("p (b t) -> p b t", b=ROW_BLOCKS))
-            turn(banks[TURN_BANKS[j]], result[j], ROW_BLOCKS)
-            pairs = held("pairs%d" % j, [P, N], BF16)
-            nc.scalar.copy(
-                out=pairs[:].rearrange("p (u m e) -> p u m e", u=2, e=2),
-                in_=banks[TURN_BANKS[j]][:].rearrange("p (m u e) -> p u m e", u=2, e=2),
-            )
-            turn(banks[WORD_BANKS[j]], pairs[:].bitcast(F32), 2)
-            nc.scalar.copy(
-                out=grouped[j][:].bitcast(F32).rearrange("p (t u) -> p t u", u=2),
-                in_=banks[WORD_BANKS[j]][:, 0 : 2 * P].rearrange("p (u t) -> p t u", u=2),
-            )
+            woven = grouped[j][:].rearrange("p (c i b) -> p c b i", i=PACK, b=PACK)
+            rows = result[j][:].rearrange("p (b c i) -> p c b i", i=PACK, b=PACK)
+            if j in VECTOR_ROUND:
+                nc.vector.tensor_copy(woven, rows)
+            else:
+                nc.scalar.copy(out=woven, in_=rows)
 
         def hand_on(j):
             tokens = slice(j * P, (j + 1) * P)
             nc.vector.quantize_mx(
                 out=out_codes[:, tokens].bitcast(FP8X4), scales=out_plane[:, tokens], in_=grouped[j][:]
             )
-            nc.sync.dma_start(out=out_words[:, tokens], in_=out_codes[:, tokens].bitcast(I32))
+            if j % 2 == 1:
+                both_tiles = slice((j - 1) * P, (j + 1) * P)
+                nc.sync.dma_start(out=out_words[:, both_tiles], in_=out_codes[:, both_tiles].bitcast(I32))
 
-        for e in range(E + 4):
-            if e < E:
-                routed_product(e)
-            if e >= 3 and e % 2 == 1:
-                for done in (e - 3, e - 2):
-                    if done < E:
-                        routed_relu(done)
-                        routed_square(done)
-                        routed_quantize(done)
-        shared_product(0)
-        shared_relu(0)
-        slot_results(0, 0)
-        slot_results(1, 0)
-        slot_results(0, 1)
-        slot_results(1, 1)
+        deal_bytes(w2_rows_dealt, w2_rows)
+        load_rest()
+        for e in range(0, E + AHEAD, 2):
+            for i in (e, e + 1):
+                if i < E:
+                    routed_product(i)
+            for i in (e, e + 1):
+                if i < E:
+                    routed_relu(i)
+            for i in (e - AHEAD, e - AHEAD + 1):
+                if i >= 0:
+                    routed_turn(i)
+        for half in range(2):
+            deal_fp4(half, 0)
+            for e in range(4 * half, 4 * half + 4):
+                routed_square(e)
+                routed_quantize(e)
+        for half in range(2):
+            deal_fp4(half, 1)
+        for b in range(0, ROW_BLOCKS, 2):
+            for half in range(2):
+                slot_results(b, half)
+                slot_results(b + 1, half)
+        for j in range(TOKEN_TILES + 1):
+            if j < TOKEN_TILES:
+                shared_product(j)
+                shared_relu(j)
+            if j > 0:
+                shared_square(j - 1)
         pick(0)
-        slot_results(2, 0)
-        slot_results(2, 1)
-        shared_square(0)
         pick(1)
-        shared_quantize(0)
-        slot_results(3, 0)
-        slot_results(3, 1)
-        shared_product(1)
-        shared_relu(1)
-        shared_square(1)
         pick(2)
+        deal_bytes(w2s_plane_dealt, w2s_plane)
+        for g in range(SHARED_PASSES):
+            deal_fp8(g)
+        shared_quantize(0)
         pick(3)
-        shared_quantize(1)
-        for j in (2, 3):
-            shared_product(j)
-            shared_relu(j)
-        for j in (2, 3):
-            shared_square(j)
+        for j in range(1, TOKEN_TILES):
             shared_quantize(j)
         for j in range(TOKEN_TILES):
             shared_out(j)
-        for pair in range(0, TOKEN_TILES, 2):
-            add_picked(pair)
-            add_picked(pair + 1)
-            finish(pair)
-            finish(pair + 1)
+        for j in range(TOKEN_TILES):
+            add_picked(j)
+        for j in range(TOKEN_TILES):
+            finish(j)
         for j in range(TOKEN_TILES):
             hand_on(j)
         for q in range(QUADS):

@@ -26,12 +26,14 @@ ROW_BLOCKS = N // P
 TOKEN_TILES = T // P
 SHARED_PASSES = HS // PASS
 LIST_ROWS = 16
-GATHER_SIZES = [1, 1, 2, 2, 2]
+WORD_GATHERS = [3, 3, 2]
+BYTE_GATHERS = [1, 1, 3, 3]
 VECTOR_RELU_EXPERTS = [4, 5, 6, 7]
 VECTOR_RELU_SHARED = []
 VECTOR_ROUND = [3]
 AHEAD = 2
-Y_BANKS = [[0, 2], [1, 3], [4, 5], [6, 7]]
+QUANTIZE_SIZES = [4, 2, 1, 1]
+LINE = 8
 SHARED_BANKS = [[0, 1], [2, 3], [4, 5], [6, 7]]
 SHARED_TURN_BANKS = [[0, 1], [2, 3], [4, 5], [6, 7]]
 YS_BANKS = [0, 4, 5, 1]
@@ -85,12 +87,12 @@ def tile_moe_shf_mlp_relu2_kernel(
         w2_rows_dealt = held("w2_rows_dealt", [P, PACK, P], U8)
         w1s_sb = [held("w1s_sb%d" % g, [P, PASS], I32) for g in range(SHARED_PASSES)]
         w2s_sb = held("w2s_sb", [P, SHARED_PASSES, N], I32)
-        gate_sb = held("gate_sb", [P, 2, T], F32)
+        gate_sb = [held("gate_sb%d" % r, [P, T], F32) for r in range(2)]
         identity = held("identity", [P, P], F32)
         w2_dealt = [
             [held("w2_dealt%d_%d" % (i, u), [P, 4, 2, 2 * P], U8) for u in range(2)] for i in range(E // 4)
         ]
-        w2s_dealt = [held("w2s_dealt%d" % g, [P, PACK, P], I32) for g in range(SHARED_PASSES)]
+        w2s_dealt = held("w2s_dealt", [P, SHARED_PASSES, PACK, P], I32)
         w2s_plane_dealt = held("w2s_plane_dealt", [P, PACK, P], U8)
 
         nc.gpsimd.memset(x_plane[:].bitcast(I32), 0)
@@ -105,45 +107,50 @@ def tile_moe_shf_mlp_relu2_kernel(
         both = (nc.sync, nc.scalar, nc.sync, nc.scalar)
         w1s_flat = w1s_words[0].rearrange("p l d -> p (l d)").bitcast(I32)
         nc.sync.dma_start(out=x_sb[:], in_=x_words[0].rearrange("p t d -> p (t d)").bitcast(I32))
-        load_rows(both, x_plane, x_scales)
         nc.sync.dma_start(offs_sb[:], offs)
+        load_rows(both, x_plane, x_scales)
         load_experts(nc.sync, w1_sb[0], w1_words, 0, 2)
         load_rows((nc.scalar, nc.scalar, nc.sync, nc.sync), w1_plane, w1_scales[:, 0])
-        nc.sync.dma_start(
-            out=w2_rows[:].bitcast(I32), in_=w2_scales[:, 0].rearrange("e b n -> b e n").bitcast(I32)
-        )
+        nc.sync.dma_start(out=w2_rows[:].bitcast(I32), in_=w2_scales[:, 0].rearrange("e b n -> b e n").bitcast(I32))
         load_experts(nc.sync, w1_sb[1], w1_words, 2, 2)
         load_experts(nc.sync, w1_sb[2], w1_words, 4, 2)
         load_experts(nc.sync, w1_sb[3], w1_words, 6, 2)
-        for i in range(E // 4):
-            load_experts(nc.sync, w2_sb[i], w2_words, 4 * i, 4)
-        load_packed_rows(sync4, w2s_plane, w2s_scales)
-        nc.sync.dma_start(out=w2s_sb[:], in_=w2s_words.rearrange("g p n d -> p g (n d)").bitcast(I32))
+        load_experts(nc.sync, w2_sb[0], w2_words, 0, 4)
+        load_experts(nc.sync, w2_sb[1], w2_words, 4, 4)
 
-        def load_rest():
+        def spread_rows():
             for q in range(QUADS):
                 nc.sync.dma_start(
                     out=w2_plane[32 * q : 32 * q + 4, :, :].bitcast(I32),
                     in_=w2_rows_dealt[32 * q : 32 * q + 32, :, :].rearrange("p t m -> p (t m)").bitcast(I32),
                 )
+
+        def load_rest():
+            spread_rows()
+            load_packed_rows(sync4, w2s_plane, w2s_scales)
+            nc.sync.dma_start(out=w2s_sb[:], in_=w2s_words.rearrange("g p n d -> p g (n d)").bitcast(I32))
             load_packed_rows(sync4, w1s_plane, w1s_scales[0].rearrange("b (g n) -> g b n", g=SHARED_PASSES))
             nc.sync.dma_start(out=w1s_sb[0][:], in_=w1s_flat[:, 0:PASS])
             nc.sync.dma_start(out=w1s_sb[1][:], in_=w1s_flat[:, PASS : 2 * PASS])
             nc.sync.dma_start(pos_sb[0][:], pos1)
             nc.sync.dma_start(pos_sb[1][:], pos2)
-            nc.sync.dma_start(out=gate_sb[:], in_=gate.rearrange("r p t -> p r t"))
+            nc.sync.dma_start(out=gate_sb[0][:], in_=gate[0])
+            nc.sync.dma_start(out=gate_sb[1][:], in_=gate[1])
 
         def deal_bytes(dealt, rows):
             nc.vector.tensor_copy(dealt[:], rows[:].rearrange("p (m t) -> p t m", t=PACK))
 
         def deal_fp4(i, u):
-            columns = w2_sb[i][:].bitcast(U16).rearrange("p e (m t) -> p e t m", t=PACK)
-            nc.vector.tensor_copy(w2_dealt[i][u][:].bitcast(U16), columns[:, :, 2 * u : 2 * u + 2, :])
-
-        def deal_fp8(g):
+            columns = w2_sb[i][:].bitcast(U16).rearrange("p e (c i t) -> p e c t i", i=LINE, t=PACK)
             nc.vector.tensor_copy(
-                w2s_dealt[g][:].rearrange("p t (c i) -> p c t i", i=PACK),
-                w2s_sb[:, g, :].rearrange("p (c i t) -> p c t i", i=PACK, t=PACK),
+                w2_dealt[i][u][:].bitcast(U16).rearrange("p e t (c i) -> p e c t i", i=LINE),
+                columns[:, :, :, 2 * u : 2 * u + 2, :],
+            )
+
+        def deal_fp8():
+            nc.vector.tensor_copy(
+                w2s_dealt[:].rearrange("p g t (c i) -> p g c t i", i=PACK),
+                w2s_sb[:].rearrange("p g (c i t) -> p g c t i", i=PACK, t=PACK),
             )
 
         def product(tokens, token_scales, weights, weight_scales, pre):
@@ -172,27 +179,36 @@ def tile_moe_shf_mlp_relu2_kernel(
                 in_=turned[:].rearrange("p (t s) -> p s t", t=PACK), func=ACT.Square,
             )
 
-        slot_words, slot_plane = [], []
-        first = 0
-        for count in GATHER_SIZES:
-            columns = offs_sb[:, first * C // LIST_ROWS : (first + count) * C // LIST_ROWS]
-            words = held("slot_words%d" % first, [P, count * C], U32)
-            plane = held("slot_plane%d" % first, [P, count * C], U8)
-            slot_words.extend([(words, plane, columns, i) for i in range(count)])
-            first = first + count
+        def gather(name, window, dtype, sizes):
+            parts, first = [], 0
+            for count in sizes:
+                columns = offs_sb[:, first * C // LIST_ROWS : (first + count) * C // LIST_ROWS]
+                gathered = held("%s%d" % (name, first), [P, count * C], dtype)
+                nc.vector.tensor_copy(gathered[:], window.indirect(columns))
+                parts.extend([gathered[:, i * C : (i + 1) * C] for i in range(count)])
+                first = first + count
+            return parts
 
-        h_codes = [held("h_codes%d" % e, [P, C], U32) for e in range(E)]
-        h_plane = [held("h_plane%d" % e, [P, C], U8) for e in range(E)]
-        rounded = [held("rounded%d" % e, [P, PASS], BF16) for e in range(E)]
+        slot_words = gather("slot_words", x_sb[:].bitcast(U32), U32, WORD_GATHERS)
+        slot_plane = gather("slot_plane", x_plane[:, 0, :], U8, BYTE_GATHERS)
+
+        h_codes, h_plane, rounded, group_of = [], [], [], {}
+        first = 0
+        for count in QUANTIZE_SIZES:
+            codes = held("h_codes%d" % first, [P, count * C], U32)
+            plane = held("h_plane%d" % first, [P, count * C], U8)
+            values = held("rounded%d" % first, [P, count * PASS], BF16)
+            for i in range(count):
+                h_codes.append(codes[:, i * C : (i + 1) * C])
+                h_plane.append(plane[:, i * C : (i + 1) * C])
+                rounded.append(values[:, i * PASS : (i + 1) * PASS])
+            first = first + count
+            group_of.setdefault(first - 1, (codes, plane, values))
         positive = {}
 
         def routed_product(e):
-            words, plane, columns, i = slot_words[e]
-            if i == 0:
-                nc.vector.tensor_copy(plane[:], x_plane[:, 0, :].indirect(columns))
-                nc.vector.tensor_copy(words[:], x_sb[:].bitcast(U32).indirect(columns))
             product(
-                words[:, i * C : (i + 1) * C].bitcast(FP8X4), plane[:, i * C : (i + 1) * C],
+                slot_words[e].bitcast(FP8X4), slot_plane[e],
                 w1_sb[e // 2][:, e % 2, :].bitcast(FP4X4), w1_plane[:, e, :], banks[e],
             )
 
@@ -203,31 +219,46 @@ def tile_moe_shf_mlp_relu2_kernel(
             turn(banks[e], positive[e], PACK)
 
         def routed_square(e):
-            square(rounded[e][:], banks[e])
+            square(rounded[e], banks[e])
 
         def routed_quantize(e):
-            nc.vector.quantize_mx(out=h_codes[e][:].bitcast(FP8X4), scales=h_plane[e][:], in_=rounded[e][:])
+            if e in group_of:
+                codes, plane, values = group_of[e]
+                nc.vector.quantize_mx(out=codes[:].bitcast(FP8X4), scales=plane[:], in_=values[:])
 
         y_sb = [held("y_sb%d" % b, [P, SLOTS], F32) for b in range(ROW_BLOCKS)]
         picked = [held("picked%d" % r, [P, ROW_BLOCKS, T], F32) for r in range(2)]
 
         def slot_results(b, half):
-            sums = banks[Y_BANKS[b][half]]
+            sums = banks[4 * (b // 2) + 2 * half + b % 2]
             for i in range(4):
                 e = 4 * half + i
                 nc.tensor.matmul_mx(
                     out=sums[:, i * C : (i + 1) * C],
                     lhsT=w2_dealt[half][b // 2][:, i, b % 2, :].bitcast(FP4X4),
                     lhsT_scale=w2_plane[:, e, b * P : (b + 1) * P],
-                    rhs=h_codes[e][:].bitcast(FP8X4), rhs_scale=h_plane[e][:],
+                    rhs=h_codes[e].bitcast(FP8X4), rhs_scale=h_plane[e],
                     start=True, stop=True,
                 )
             nc.scalar.copy(out=y_sb[b][:, half * PASS : (half + 1) * PASS], in_=sums[:])
 
+        def first_block_end():
+            for bank, experts in ((2, range(4, E - 1)), (7, range(E - 1, E))):
+                for e in experts:
+                    nc.tensor.matmul_mx(
+                        out=banks[bank][:, (e - 4) * C : (e - 3) * C],
+                        lhsT=w2_dealt[1][0][:, e - 4, 0, :].bitcast(FP4X4), lhsT_scale=w2_plane[:, e, 0:P],
+                        rhs=h_codes[e].bitcast(FP8X4), rhs_scale=h_plane[e], start=True, stop=True,
+                    )
+                first, last = experts[0], experts[-1] + 1
+                nc.scalar.copy(
+                    out=y_sb[0][:, first * C : last * C], in_=banks[bank][:, (first - 4) * C : (last - 4) * C]
+                )
+
         def pick(b):
             for r in range(2):
                 nc.vector.tensor_tensor(
-                    picked[r][:, b, :], y_sb[b][:].indirect(pos_sb[r][:]), gate_sb[:, r, :], ALU.mult
+                    picked[r][:, b, :], y_sb[b][:].indirect(pos_sb[r][:]), gate_sb[r][:], ALU.mult
                 )
 
         rounded_s = [held("rounded_s%d" % j, [P, SHARED_PASSES * PASS], BF16) for j in range(TOKEN_TILES)]
@@ -265,7 +296,7 @@ def tile_moe_shf_mlp_relu2_kernel(
                 for g in range(SHARED_PASSES):
                     nc.tensor.matmul_mx(
                         out=sums[:, b * P : (b + 1) * P],
-                        lhsT=w2s_dealt[g][:, b, :].bitcast(FP8X4),
+                        lhsT=w2s_dealt[:, g, b, :].bitcast(FP8X4),
                         lhsT_scale=w2s_plane_dealt[4 * g :, b, :],
                         rhs=hs_codes[j][:, g * P : (g + 1) * P].bitcast(FP8X4),
                         rhs_scale=hs_plane[j][:, g * P : (g + 1) * P],
@@ -325,10 +356,13 @@ def tile_moe_shf_mlp_relu2_kernel(
                 routed_quantize(e)
         for half in range(2):
             deal_fp4(half, 1)
-        for b in range(0, ROW_BLOCKS, 2):
-            for half in range(2):
-                slot_results(b, half)
-                slot_results(b + 1, half)
+        slot_results(0, 0)
+        first_block_end()
+        slot_results(1, 0)
+        slot_results(1, 1)
+        for half in range(2):
+            slot_results(2, half)
+            slot_results(3, half)
         for j in range(TOKEN_TILES + 1):
             if j < TOKEN_TILES:
                 shared_product(j)
@@ -339,8 +373,7 @@ def tile_moe_shf_mlp_relu2_kernel(
         pick(1)
         pick(2)
         deal_bytes(w2s_plane_dealt, w2s_plane)
-        for g in range(SHARED_PASSES):
-            deal_fp8(g)
+        deal_fp8()
         shared_quantize(0)
         pick(3)
         for j in range(1, TOKEN_TILES):

@@ -20,22 +20,19 @@ ALU = mybir.AluOpType
 P = 128
 PACK = 4
 QUADS = 4
+SCALE_ROWS = 4
 PASS = P * PACK
 SLOTS = E * C
 ROW_BLOCKS = N // P
 TOKEN_TILES = T // P
 SHARED_PASSES = HS // PASS
+HALF = E // 2
 LIST_ROWS = 16
-WORD_GATHERS = [3, 3, 2]
-BYTE_GATHERS = [1, 1, 3, 3]
-VECTOR_RELU_EXPERTS = [4, 5, 6, 7]
-VECTOR_RELU_SHARED = []
-VECTOR_ROUND = [3]
-AHEAD = 2
-QUANTIZE_SIZES = [4, 2, 1, 1]
 LINE = 8
-SHARED_BANKS = [[0, 1], [2, 3], [4, 5], [6, 7]]
-SHARED_TURN_BANKS = [[0, 1], [2, 3], [4, 5], [6, 7]]
+GATHER_SIZES = [1, 1, 2, 2, 2]
+QUANTIZE_SIZES = [4, 2, 1, 1]
+FIRST_VECTOR_RELU = 5
+AHEAD = 2
 YS_BANKS = [0, 4, 5, 1]
 
 
@@ -54,21 +51,21 @@ def tile_moe_shf_mlp_relu2_kernel(
         banks = [psum.tile([P, PASS], F32, name="bank%d" % i) for i in range(8)]
 
         def load_rows(queues, plane, scales):
-            for r in range(4):
+            for r in range(SCALE_ROWS):
                 queues[r].dma_start(
                     out=plane[r:P:32, :, :].bitcast(I32),
-                    in_=scales[:, r:16:4, :].rearrange("g q n -> q g n").bitcast(I32),
+                    in_=scales[:, r:16:SCALE_ROWS, :].rearrange("g q n -> q g n").bitcast(I32),
                 )
 
-        def load_packed_rows(queues, plane, scales):
+        def load_packed_rows(plane, scales):
             for q in range(QUADS):
-                queues[q].dma_start(
-                    out=plane[32 * q : 32 * q + 4 * SHARED_PASSES, :].bitcast(I32),
-                    in_=scales[:, 4 * q : 4 * q + 4, :].bitcast(I32),
+                nc.sync.dma_start(
+                    out=plane[32 * q : 32 * q + SCALE_ROWS * SHARED_PASSES, :].bitcast(I32),
+                    in_=scales[:, SCALE_ROWS * q : SCALE_ROWS * (q + 1), :].bitcast(I32),
                 )
 
-        def load_experts(queue, tile, words, first, count):
-            queue.dma_start(
+        def load_experts(tile, words, first, count):
+            nc.sync.dma_start(
                 out=tile[:].bitcast(I32),
                 in_=words[first : first + count, 0].rearrange("e p n -> p e n").bitcast(I32),
             )
@@ -82,240 +79,229 @@ def tile_moe_shf_mlp_relu2_kernel(
         w1s_plane = held("w1s_plane", [P, PASS], U8)
         w2s_plane = held("w2s_plane", [P, N], U8)
         w1_sb = [held("w1_sb%d" % i, [P, 2, 2 * H], U8) for i in range(E // 2)]
-        w2_sb = [held("w2_sb%d" % i, [P, 4, 2 * N], U8) for i in range(E // 4)]
+        w2_sb = [held("w2_sb%d" % i, [P, HALF, 2 * N], U8) for i in range(2)]
         w2_rows = held("w2_rows", [P, N], U8)
         w2_rows_dealt = held("w2_rows_dealt", [P, PACK, P], U8)
         w1s_sb = [held("w1s_sb%d" % g, [P, PASS], I32) for g in range(SHARED_PASSES)]
         w2s_sb = held("w2s_sb", [P, SHARED_PASSES, N], I32)
-        gate_sb = [held("gate_sb%d" % r, [P, T], F32) for r in range(2)]
+        gate_sb = held("gate_sb", [P, 2, T], F32)
         identity = held("identity", [P, P], F32)
-        w2_dealt = [
-            [held("w2_dealt%d_%d" % (i, u), [P, 4, 2, 2 * P], U8) for u in range(2)] for i in range(E // 4)
-        ]
+        w2_dealt = [[held("w2_dealt%d_%d" % (i, u), [P, HALF, 2, 2 * P], U8) for u in range(2)] for i in range(2)]
         w2s_dealt = held("w2s_dealt", [P, SHARED_PASSES, PACK, P], I32)
         w2s_plane_dealt = held("w2s_plane_dealt", [P, PACK, P], U8)
 
         nc.gpsimd.memset(x_plane[:].bitcast(I32), 0)
-        nc.gpsimd.memset(w1_plane[:, 0 : E // 2, :].bitcast(I32), 0)
-        nc.vector.memset(w1_plane[:, E // 2 : E, :].bitcast(I32), 0)
+        nc.gpsimd.memset(w1_plane[:, 0:HALF, :].bitcast(I32), 0)
+        nc.vector.memset(w1_plane[:, HALF:E, :].bitcast(I32), 0)
         nc.vector.memset(w1s_plane[:].bitcast(I32), 0)
         nc.vector.memset(w2_plane[:].bitcast(I32), 0)
         make_identity(nc, identity[:])
         nc.gpsimd.memset(w2s_plane[:].bitcast(I32), 0)
 
-        sync4 = (nc.sync,) * 4
-        both = (nc.sync, nc.scalar, nc.sync, nc.scalar)
-        w1s_flat = w1s_words[0].rearrange("p l d -> p (l d)").bitcast(I32)
         nc.sync.dma_start(out=x_sb[:], in_=x_words[0].rearrange("p t d -> p (t d)").bitcast(I32))
+        load_rows((nc.sync, nc.scalar, nc.sync, nc.scalar), x_plane, x_scales)
         nc.sync.dma_start(offs_sb[:], offs)
-        load_rows(both, x_plane, x_scales)
-        load_experts(nc.sync, w1_sb[0], w1_words, 0, 2)
+        load_experts(w1_sb[0], w1_words, 0, 2)
         load_rows((nc.scalar, nc.scalar, nc.sync, nc.sync), w1_plane, w1_scales[:, 0])
         nc.sync.dma_start(out=w2_rows[:].bitcast(I32), in_=w2_scales[:, 0].rearrange("e b n -> b e n").bitcast(I32))
-        load_experts(nc.sync, w1_sb[1], w1_words, 2, 2)
-        load_experts(nc.sync, w1_sb[2], w1_words, 4, 2)
-        load_experts(nc.sync, w1_sb[3], w1_words, 6, 2)
-        load_experts(nc.sync, w2_sb[0], w2_words, 0, 4)
-        load_experts(nc.sync, w2_sb[1], w2_words, 4, 4)
-
-        def spread_rows():
-            for q in range(QUADS):
-                nc.sync.dma_start(
-                    out=w2_plane[32 * q : 32 * q + 4, :, :].bitcast(I32),
-                    in_=w2_rows_dealt[32 * q : 32 * q + 32, :, :].rearrange("p t m -> p (t m)").bitcast(I32),
-                )
-
-        def load_rest():
-            spread_rows()
-            load_packed_rows(sync4, w2s_plane, w2s_scales)
-            nc.sync.dma_start(out=w2s_sb[:], in_=w2s_words.rearrange("g p n d -> p g (n d)").bitcast(I32))
-            load_packed_rows(sync4, w1s_plane, w1s_scales[0].rearrange("b (g n) -> g b n", g=SHARED_PASSES))
-            nc.sync.dma_start(out=w1s_sb[0][:], in_=w1s_flat[:, 0:PASS])
-            nc.sync.dma_start(out=w1s_sb[1][:], in_=w1s_flat[:, PASS : 2 * PASS])
-            nc.sync.dma_start(pos_sb[0][:], pos1)
-            nc.sync.dma_start(pos_sb[1][:], pos2)
-            nc.sync.dma_start(out=gate_sb[0][:], in_=gate[0])
-            nc.sync.dma_start(out=gate_sb[1][:], in_=gate[1])
+        for i in range(1, E // 2):
+            load_experts(w1_sb[i], w1_words, 2 * i, 2)
+        for half in range(2):
+            load_experts(w2_sb[half], w2_words, HALF * half, HALF)
+        load_packed_rows(w2s_plane, w2s_scales)
+        nc.sync.dma_start(out=w2s_sb[:], in_=w2s_words.rearrange("g p n d -> p g (n d)").bitcast(I32))
 
         def deal_bytes(dealt, rows):
-            nc.vector.tensor_copy(dealt[:], rows[:].rearrange("p (m t) -> p t m", t=PACK))
+            nc.vector.tensor_copy(dealt[:], rows[:].rearrange("p (m d) -> p d m", d=PACK))
 
-        def deal_fp4(i, u):
-            columns = w2_sb[i][:].bitcast(U16).rearrange("p e (c i t) -> p e c t i", i=LINE, t=PACK)
+        def deal_fp4(half, pair):
+            columns = w2_sb[half][:].bitcast(U16).rearrange("p e (c i d) -> p e c d i", i=LINE, d=PACK)
             nc.vector.tensor_copy(
-                w2_dealt[i][u][:].bitcast(U16).rearrange("p e t (c i) -> p e c t i", i=LINE),
-                columns[:, :, :, 2 * u : 2 * u + 2, :],
+                w2_dealt[half][pair][:].bitcast(U16).rearrange("p e d (c i) -> p e c d i", i=LINE),
+                columns[:, :, :, 2 * pair : 2 * pair + 2, :],
             )
 
-        def deal_fp8():
-            nc.vector.tensor_copy(
-                w2s_dealt[:].rearrange("p g t (c i) -> p g c t i", i=PACK),
-                w2s_sb[:].rearrange("p g (c i t) -> p g c t i", i=PACK, t=PACK),
-            )
-
-        def product(tokens, token_scales, weights, weight_scales, pre):
+        def product(tokens, token_scales, weights, weight_scales, bank):
             nc.tensor.matmul_mx(
-                out=pre[:], lhsT=tokens, lhsT_scale=token_scales, rhs=weights, rhs_scale=weight_scales,
+                out=bank[:], lhsT=tokens, lhsT_scale=token_scales, rhs=weights, rhs_scale=weight_scales,
                 start=True, stop=True,
             )
 
-        def relu(pre, on_vector, name):
+        def relu(bank, name, on_vector):
             positive = held(name, [P, PASS], F32)
-            dealt = pre[:].rearrange("p (m t) -> p t m", t=PACK)
-            target = positive[:].rearrange("p (t m) -> p t m", t=PACK)
+            dealt = bank[:].rearrange("p (m d) -> p d m", d=PACK)
+            target = positive[:].rearrange("p (d m) -> p d m", d=PACK)
             if on_vector:
                 nc.vector.tensor_scalar(out=target, in0=dealt, scalar1=0.0, scalar2=None, op0=ALU.max)
             else:
                 nc.scalar.activation(out=target, in_=dealt, func=ACT.Relu)
             return positive
 
-        def turn(turned, source, count):
-            for t in range(count):
-                nc.tensor.transpose(turned[:, t * P : (t + 1) * P], source[:, t * P : (t + 1) * P], identity[:])
+        def turn(bank, positive):
+            for d in range(PACK):
+                nc.tensor.transpose(bank[:, d * P : (d + 1) * P], positive[:, d * P : (d + 1) * P], identity[:])
 
-        def square(rounded, turned):
+        def square(target, bank):
             nc.scalar.activation(
-                out=rounded.rearrange("p (s t) -> p s t", t=PACK),
-                in_=turned[:].rearrange("p (t s) -> p s t", t=PACK), func=ACT.Square,
+                out=target.rearrange("p (s d) -> p s d", d=PACK),
+                in_=bank[:].rearrange("p (d s) -> p s d", d=PACK), func=ACT.Square,
             )
 
-        def gather(name, window, dtype, sizes):
-            parts, first = [], 0
-            for count in sizes:
-                columns = offs_sb[:, first * C // LIST_ROWS : (first + count) * C // LIST_ROWS]
-                gathered = held("%s%d" % (name, first), [P, count * C], dtype)
-                nc.vector.tensor_copy(gathered[:], window.indirect(columns))
-                parts.extend([gathered[:, i * C : (i + 1) * C] for i in range(count)])
-                first = first + count
-            return parts
+        slot_words, slot_plane = [], []
+        first = 0
+        for count in GATHER_SIZES:
+            columns = offs_sb[:, first * C // LIST_ROWS : (first + count) * C // LIST_ROWS]
+            plane = held("slot_plane%d" % first, [P, count * C], U8)
+            words = held("slot_words%d" % first, [P, count * C], U32)
+            nc.vector.tensor_copy(plane[:], x_plane[:, 0, :].indirect(columns))
+            nc.vector.tensor_copy(words[:], x_sb[:].bitcast(U32).indirect(columns))
+            slot_plane.extend([plane[:, i * C : (i + 1) * C] for i in range(count)])
+            slot_words.extend([words[:, i * C : (i + 1) * C] for i in range(count)])
+            first = first + count
 
-        slot_words = gather("slot_words", x_sb[:].bitcast(U32), U32, WORD_GATHERS)
-        slot_plane = gather("slot_plane", x_plane[:, 0, :], U8, BYTE_GATHERS)
-
-        h_codes, h_plane, rounded, group_of = [], [], [], {}
+        h_codes, h_plane, rounded, group_ending_at = [], [], [], {}
         first = 0
         for count in QUANTIZE_SIZES:
             codes = held("h_codes%d" % first, [P, count * C], U32)
             plane = held("h_plane%d" % first, [P, count * C], U8)
             values = held("rounded%d" % first, [P, count * PASS], BF16)
-            for i in range(count):
-                h_codes.append(codes[:, i * C : (i + 1) * C])
-                h_plane.append(plane[:, i * C : (i + 1) * C])
-                rounded.append(values[:, i * PASS : (i + 1) * PASS])
+            h_codes.extend([codes[:, i * C : (i + 1) * C] for i in range(count)])
+            h_plane.extend([plane[:, i * C : (i + 1) * C] for i in range(count)])
+            rounded.extend([values[:, i * PASS : (i + 1) * PASS] for i in range(count)])
             first = first + count
-            group_of.setdefault(first - 1, (codes, plane, values))
-        positive = {}
-
-        def routed_product(e):
-            product(
-                slot_words[e].bitcast(FP8X4), slot_plane[e],
-                w1_sb[e // 2][:, e % 2, :].bitcast(FP4X4), w1_plane[:, e, :], banks[e],
-            )
-
-        def routed_relu(e):
-            positive.setdefault(e, relu(banks[e], e in VECTOR_RELU_EXPERTS, "positive%d" % e))
-
-        def routed_turn(e):
-            turn(banks[e], positive[e], PACK)
-
-        def routed_square(e):
-            square(rounded[e], banks[e])
-
-        def routed_quantize(e):
-            if e in group_of:
-                codes, plane, values = group_of[e]
-                nc.vector.quantize_mx(out=codes[:].bitcast(FP8X4), scales=plane[:], in_=values[:])
+            group_ending_at.setdefault(first - 1, (codes, plane, values))
 
         y_sb = [held("y_sb%d" % b, [P, SLOTS], F32) for b in range(ROW_BLOCKS)]
         picked = [held("picked%d" % r, [P, ROW_BLOCKS, T], F32) for r in range(2)]
+        rounded_s = [held("rounded_s%d" % j, [P, SHARED_PASSES * PASS], BF16) for j in range(TOKEN_TILES)]
+        hs_codes = [held("hs_codes%d" % j, [P, SHARED_PASSES * P], U32) for j in range(TOKEN_TILES)]
+        hs_plane = [held("hs_plane%d" % j, [P, SHARED_PASSES * P], U8) for j in range(TOKEN_TILES)]
+        out_codes = held("out_codes", [P, T], U32)
+        out_plane = held("out_plane", [P, T], U8)
+        routed = [held("routed%d" % j, [P, ROW_BLOCKS, P], F32) for j in range(TOKEN_TILES)]
+        result = [held("result%d" % j, [P, ROW_BLOCKS * P], F32) for j in range(TOKEN_TILES)]
+        grouped = [held("grouped%d" % j, [P, PACK * P], BF16) for j in range(TOKEN_TILES)]
+        out_rows = out_0.rearrange("(p b) t -> p b t", p=P)
+        out_words = out_1[0].rearrange("p t d -> p (t d)").bitcast(I32)
 
-        def slot_results(b, half):
-            sums = banks[4 * (b // 2) + 2 * half + b % 2]
-            for i in range(4):
-                e = 4 * half + i
+        def slot_results(b, first_expert, end_expert, bank):
+            half = first_expert // HALF
+            for e in range(first_expert, end_expert):
+                i = e % HALF
                 nc.tensor.matmul_mx(
-                    out=sums[:, i * C : (i + 1) * C],
+                    out=bank[:, i * C : (i + 1) * C],
                     lhsT=w2_dealt[half][b // 2][:, i, b % 2, :].bitcast(FP4X4),
                     lhsT_scale=w2_plane[:, e, b * P : (b + 1) * P],
                     rhs=h_codes[e].bitcast(FP8X4), rhs_scale=h_plane[e],
                     start=True, stop=True,
                 )
-            nc.scalar.copy(out=y_sb[b][:, half * PASS : (half + 1) * PASS], in_=sums[:])
+            nc.scalar.copy(
+                out=y_sb[b][:, first_expert * C : end_expert * C],
+                in_=bank[:, (first_expert - HALF * half) * C : (end_expert - HALF * half) * C],
+            )
 
-        def first_block_end():
-            for bank, experts in ((2, range(4, E - 1)), (7, range(E - 1, E))):
-                for e in experts:
-                    nc.tensor.matmul_mx(
-                        out=banks[bank][:, (e - 4) * C : (e - 3) * C],
-                        lhsT=w2_dealt[1][0][:, e - 4, 0, :].bitcast(FP4X4), lhsT_scale=w2_plane[:, e, 0:P],
-                        rhs=h_codes[e].bitcast(FP8X4), rhs_scale=h_plane[e], start=True, stop=True,
-                    )
-                first, last = experts[0], experts[-1] + 1
-                nc.scalar.copy(
-                    out=y_sb[0][:, first * C : last * C], in_=banks[bank][:, (first - 4) * C : (last - 4) * C]
-                )
+        def half_results(b, half):
+            slot_results(b, HALF * half, HALF * (half + 1), banks[4 * (b // 2) + 2 * half + b % 2])
 
         def pick(b):
             for r in range(2):
                 nc.vector.tensor_tensor(
-                    picked[r][:, b, :], y_sb[b][:].indirect(pos_sb[r][:]), gate_sb[r][:], ALU.mult
+                    picked[r][:, b, :], y_sb[b][:].indirect(pos_sb[r][:]), gate_sb[:, r, :], ALU.mult
                 )
-
-        rounded_s = [held("rounded_s%d" % j, [P, SHARED_PASSES * PASS], BF16) for j in range(TOKEN_TILES)]
-        hs_codes = [held("hs_codes%d" % j, [P, SHARED_PASSES * P], U32) for j in range(TOKEN_TILES)]
-        hs_plane = [held("hs_plane%d" % j, [P, SHARED_PASSES * P], U8) for j in range(TOKEN_TILES)]
-
-        kept = {}
-
-        def shared_product(j):
-            tokens = slice(j * P, (j + 1) * P)
-            for g in range(SHARED_PASSES):
-                product(
-                    x_sb[:, tokens].bitcast(FP8X4), x_plane[:, 0, tokens],
-                    w1s_sb[g][:].bitcast(FP8X4), w1s_plane[4 * g :, :], banks[SHARED_BANKS[j][g]],
-                )
-
-        def shared_relu(j):
-            kept.setdefault(j, [
-                relu(banks[SHARED_BANKS[j][g]], SHARED_PASSES * j + g in VECTOR_RELU_SHARED, "positive_s%d_%d" % (j, g))
-                for g in range(SHARED_PASSES)
-            ])
-
-        def shared_square(j):
-            for g in range(SHARED_PASSES):
-                turn(banks[SHARED_TURN_BANKS[j][g]], kept[j][g], PACK)
-            for g in range(SHARED_PASSES):
-                square(rounded_s[j][:, g * PASS : (g + 1) * PASS], banks[SHARED_TURN_BANKS[j][g]])
 
         def shared_quantize(j):
             nc.vector.quantize_mx(out=hs_codes[j][:].bitcast(FP8X4), scales=hs_plane[j][:], in_=rounded_s[j][:])
 
-        def shared_out(j):
-            sums = banks[YS_BANKS[j]]
+        deal_bytes(w2_rows_dealt, w2_rows)
+        for q in range(QUADS):
+            nc.sync.dma_start(
+                out=w2_plane[32 * q : 32 * q + SCALE_ROWS, :, :].bitcast(I32),
+                in_=w2_rows_dealt[32 * q : 32 * q + 32, :, :].rearrange("p d m -> p (d m)").bitcast(I32),
+            )
+        load_packed_rows(w1s_plane, w1s_scales[0].rearrange("b (g n) -> g b n", g=SHARED_PASSES))
+        w1s_flat = w1s_words[0].rearrange("p l d -> p (l d)").bitcast(I32)
+        for g in range(SHARED_PASSES):
+            nc.sync.dma_start(out=w1s_sb[g][:], in_=w1s_flat[:, g * PASS : (g + 1) * PASS])
+        for r, pos in enumerate((pos1, pos2)):
+            nc.sync.dma_start(pos_sb[r][:], pos)
+        nc.sync.dma_start(out=gate_sb[:], in_=gate.rearrange("r p t -> p r t"))
+
+        positive = []
+        for pair in range(0, E + AHEAD, 2):
+            for e in range(pair, min(pair + 2, E)):
+                product(
+                    slot_words[e].bitcast(FP8X4), slot_plane[e],
+                    w1_sb[e // 2][:, e % 2, :].bitcast(FP4X4), w1_plane[:, e, :], banks[e],
+                )
+            for e in range(pair, min(pair + 2, E)):
+                positive.append(relu(banks[e], "positive%d" % e, e >= FIRST_VECTOR_RELU))
+            for e in range(max(pair - AHEAD, 0), pair - AHEAD + 2):
+                turn(banks[e], positive[e])
+        for half in range(2):
+            deal_fp4(half, 0)
+            for e in range(HALF * half, HALF * (half + 1)):
+                square(rounded[e], banks[e])
+                if e in group_ending_at:
+                    codes, plane, values = group_ending_at[e]
+                    nc.vector.quantize_mx(out=codes[:].bitcast(FP8X4), scales=plane[:], in_=values[:])
+        for half in range(2):
+            deal_fp4(half, 1)
+
+        half_results(0, 0)
+        slot_results(0, HALF, E - 1, banks[2])
+        slot_results(0, E - 1, E, banks[E - 1])
+        for half in range(2):
+            half_results(1, half)
+        for half in range(2):
+            half_results(2, half)
+            half_results(3, half)
+
+        positive_s = []
+        for j in range(TOKEN_TILES + 1):
+            if j < TOKEN_TILES:
+                tokens = slice(j * P, (j + 1) * P)
+                for g in range(SHARED_PASSES):
+                    product(
+                        x_sb[:, tokens].bitcast(FP8X4), x_plane[:, 0, tokens],
+                        w1s_sb[g][:].bitcast(FP8X4), w1s_plane[SCALE_ROWS * g :, :], banks[2 * j + g],
+                    )
+                positive_s.append(
+                    [relu(banks[2 * j + g], "positive_s%d_%d" % (j, g), False) for g in range(SHARED_PASSES)]
+                )
+            if j > 0:
+                for g in range(SHARED_PASSES):
+                    turn(banks[2 * (j - 1) + g], positive_s[j - 1][g])
+                for g in range(SHARED_PASSES):
+                    square(rounded_s[j - 1][:, g * PASS : (g + 1) * PASS], banks[2 * (j - 1) + g])
+
+        for b in range(ROW_BLOCKS - 1):
+            pick(b)
+        deal_bytes(w2s_plane_dealt, w2s_plane)
+        nc.vector.tensor_copy(
+            w2s_dealt[:].rearrange("p g d (c i) -> p g c d i", i=PACK),
+            w2s_sb[:].rearrange("p g (c i d) -> p g c d i", i=PACK, d=PACK),
+        )
+        shared_quantize(0)
+        pick(ROW_BLOCKS - 1)
+        for j in range(1, TOKEN_TILES):
+            shared_quantize(j)
+
+        for j in range(TOKEN_TILES):
             for b in range(ROW_BLOCKS):
                 for g in range(SHARED_PASSES):
                     nc.tensor.matmul_mx(
-                        out=sums[:, b * P : (b + 1) * P],
+                        out=banks[YS_BANKS[j]][:, b * P : (b + 1) * P],
                         lhsT=w2s_dealt[:, g, b, :].bitcast(FP8X4),
-                        lhsT_scale=w2s_plane_dealt[4 * g :, b, :],
+                        lhsT_scale=w2s_plane_dealt[SCALE_ROWS * g :, b, :],
                         rhs=hs_codes[j][:, g * P : (g + 1) * P].bitcast(FP8X4),
                         rhs_scale=hs_plane[j][:, g * P : (g + 1) * P],
                         start=(g == 0), stop=(g == SHARED_PASSES - 1),
                     )
 
-        out_codes = held("out_codes", [P, T], U32)
-        out_plane = held("out_plane", [P, T], U8)
-        out_rows = out_0.rearrange("(p b) t -> p b t", p=P)
-        out_words = out_1[0].rearrange("p t d -> p (t d)").bitcast(I32)
-        routed = [held("routed%d" % j, [P, ROW_BLOCKS, P], F32) for j in range(TOKEN_TILES)]
-        result = [held("result%d" % j, [P, ROW_BLOCKS * P], F32) for j in range(TOKEN_TILES)]
-        grouped = [held("grouped%d" % j, [P, PACK * P], BF16) for j in range(TOKEN_TILES)]
-
-        def add_picked(j):
+        for j in range(TOKEN_TILES):
             tokens = slice(j * P, (j + 1) * P)
             nc.vector.tensor_tensor(routed[j][:], picked[0][:, :, tokens], picked[1][:, :, tokens], ALU.add)
-
-        def finish(j):
+        for j in range(TOKEN_TILES):
             tokens = slice(j * P, (j + 1) * P)
             nc.vector.tensor_tensor(
                 result[j][:], banks[YS_BANKS[j]][:], routed[j][:].rearrange("p b t -> p (b t)"), ALU.add
@@ -323,12 +309,11 @@ def tile_moe_shf_mlp_relu2_kernel(
             nc.sync.dma_start(out=out_rows[:, :, tokens], in_=result[j][:].rearrange("p (b t) -> p b t", b=ROW_BLOCKS))
             woven = grouped[j][:].rearrange("p (c i b) -> p c b i", i=PACK, b=PACK)
             rows = result[j][:].rearrange("p (b c i) -> p c b i", i=PACK, b=PACK)
-            if j in VECTOR_ROUND:
+            if j == TOKEN_TILES - 1:
                 nc.vector.tensor_copy(woven, rows)
             else:
                 nc.scalar.copy(out=woven, in_=rows)
-
-        def hand_on(j):
+        for j in range(TOKEN_TILES):
             tokens = slice(j * P, (j + 1) * P)
             nc.vector.quantize_mx(
                 out=out_codes[:, tokens].bitcast(FP8X4), scales=out_plane[:, tokens], in_=grouped[j][:]
@@ -336,58 +321,8 @@ def tile_moe_shf_mlp_relu2_kernel(
             if j % 2 == 1:
                 both_tiles = slice((j - 1) * P, (j + 1) * P)
                 nc.sync.dma_start(out=out_words[:, both_tiles], in_=out_codes[:, both_tiles].bitcast(I32))
-
-        deal_bytes(w2_rows_dealt, w2_rows)
-        load_rest()
-        for e in range(0, E + AHEAD, 2):
-            for i in (e, e + 1):
-                if i < E:
-                    routed_product(i)
-            for i in (e, e + 1):
-                if i < E:
-                    routed_relu(i)
-            for i in (e - AHEAD, e - AHEAD + 1):
-                if i >= 0:
-                    routed_turn(i)
-        for half in range(2):
-            deal_fp4(half, 0)
-            for e in range(4 * half, 4 * half + 4):
-                routed_square(e)
-                routed_quantize(e)
-        for half in range(2):
-            deal_fp4(half, 1)
-        slot_results(0, 0)
-        first_block_end()
-        slot_results(1, 0)
-        slot_results(1, 1)
-        for half in range(2):
-            slot_results(2, half)
-            slot_results(3, half)
-        for j in range(TOKEN_TILES + 1):
-            if j < TOKEN_TILES:
-                shared_product(j)
-                shared_relu(j)
-            if j > 0:
-                shared_square(j - 1)
-        pick(0)
-        pick(1)
-        pick(2)
-        deal_bytes(w2s_plane_dealt, w2s_plane)
-        deal_fp8()
-        shared_quantize(0)
-        pick(3)
-        for j in range(1, TOKEN_TILES):
-            shared_quantize(j)
-        for j in range(TOKEN_TILES):
-            shared_out(j)
-        for j in range(TOKEN_TILES):
-            add_picked(j)
-        for j in range(TOKEN_TILES):
-            finish(j)
-        for j in range(TOKEN_TILES):
-            hand_on(j)
         for q in range(QUADS):
             (nc.sync, nc.scalar)[q % 2].dma_start(
-                out=out_2[0, 4 * q : 4 * q + 4, :].bitcast(I32),
-                in_=out_plane[32 * q : 32 * q + 4, :].bitcast(I32),
+                out=out_2[0, SCALE_ROWS * q : SCALE_ROWS * (q + 1), :].bitcast(I32),
+                in_=out_plane[32 * q : 32 * q + SCALE_ROWS, :].bitcast(I32),
             )

@@ -29,7 +29,8 @@ SHARED_PASSES = HS // PASS
 HALF = E // 2
 LIST_ROWS = 16
 LINE = 8
-GATHER_SIZES = [1, 1, 2, 2, 2]
+GATHER_SIZES = [(2, (1, 1)), (3, (2, 2)), (3, (2,))]
+W1_LOADS = [2, 2, 4]
 QUANTIZE_SIZES = [4, 2, 1, 1]
 FIRST_VECTOR_RELU = 5
 AHEAD = 2
@@ -45,8 +46,8 @@ def tile_moe_shf_mlp_relu2_kernel(
         keep = ctx.enter_context(tc.tile_pool(name="keep", bufs=1))
         psum = ctx.enter_context(tc.psum_pool(name="psum", bufs=1))
 
-        def held(name, shape, dtype):
-            return keep.tile(shape, dtype, name=name, align_bytes=64)
+        def held(name, shape, dtype, tag=None):
+            return keep.tile(shape, dtype, name=name, tag=tag or name, align_bytes=64)
 
         banks = [psum.tile([P, PASS], F32, name="bank%d" % i) for i in range(8)]
 
@@ -74,15 +75,16 @@ def tile_moe_shf_mlp_relu2_kernel(
         pos_sb = [keep.tile([P, T // LIST_ROWS], U16, name="pos%d_sb" % r) for r in range(2)]
         x_sb = held("x_sb", [P, T], I32)
         x_plane = held("x_plane", [P, 1, T], U8)
-        w1_plane = held("w1_plane", [P, E, H], U8)
+        w1_plane = [held("w1_plane%d" % i, [P, HALF, H], U8) for i in range(2)]
         w2_plane = held("w2_plane", [P, E, N], U8)
         w1s_plane = held("w1s_plane", [P, PASS], U8)
         w2s_plane = held("w2s_plane", [P, N], U8)
-        w1_sb = [held("w1_sb%d" % i, [P, 2, 2 * H], U8) for i in range(E // 2)]
+        w1_sb = [held("w1_sb%d" % i, [P, count, 2 * H], U8) for i, count in enumerate(W1_LOADS)]
+        w1_of = [w1_sb[i][:, u, :] for i, count in enumerate(W1_LOADS) for u in range(count)]
         w2_sb = [held("w2_sb%d" % i, [P, HALF, 2 * N], U8) for i in range(2)]
         w2_rows = held("w2_rows", [P, N], U8)
         w2_rows_dealt = held("w2_rows_dealt", [P, PACK, P], U8)
-        w1s_sb = [held("w1s_sb%d" % g, [P, PASS], I32) for g in range(SHARED_PASSES)]
+        w1s_sb = held("w1s_sb", [P, HS], I32)
         w2s_sb = held("w2s_sb", [P, SHARED_PASSES, N], I32)
         gate_sb = held("gate_sb", [P, 2, T], F32)
         identity = held("identity", [P, P], F32)
@@ -91,21 +93,22 @@ def tile_moe_shf_mlp_relu2_kernel(
         w2s_plane_dealt = held("w2s_plane_dealt", [P, PACK, P], U8)
 
         nc.gpsimd.memset(x_plane[:].bitcast(I32), 0)
-        nc.gpsimd.memset(w1_plane[:, 0:HALF, :].bitcast(I32), 0)
-        nc.vector.memset(w1_plane[:, HALF:E, :].bitcast(I32), 0)
-        nc.vector.memset(w1s_plane[:].bitcast(I32), 0)
+        for half in range(2):
+            nc.vector.memset(w1_plane[half][:].bitcast(I32), 0)
         nc.vector.memset(w2_plane[:].bitcast(I32), 0)
         make_identity(nc, identity[:])
         nc.gpsimd.memset(w2s_plane[:].bitcast(I32), 0)
+        nc.gpsimd.memset(w1s_plane[:].bitcast(I32), 0)
 
-        nc.sync.dma_start(out=x_sb[:], in_=x_words[0].rearrange("p t d -> p (t d)").bitcast(I32))
-        load_rows((nc.sync, nc.scalar, nc.sync, nc.scalar), x_plane, x_scales)
         nc.sync.dma_start(offs_sb[:], offs)
+        load_rows((nc.sync, nc.sync, nc.scalar, nc.scalar), x_plane, x_scales)
+        nc.sync.dma_start(out=x_sb[:], in_=x_words[0].rearrange("p t d -> p (t d)").bitcast(I32))
         load_experts(w1_sb[0], w1_words, 0, 2)
-        load_rows((nc.scalar, nc.scalar, nc.sync, nc.sync), w1_plane, w1_scales[:, 0])
+        load_rows((nc.sync,) * SCALE_ROWS, w1_plane[0], w1_scales[0:HALF, 0])
+        load_experts(w1_sb[1], w1_words, 2, 2)
         nc.sync.dma_start(out=w2_rows[:].bitcast(I32), in_=w2_scales[:, 0].rearrange("e b n -> b e n").bitcast(I32))
-        for i in range(1, E // 2):
-            load_experts(w1_sb[i], w1_words, 2 * i, 2)
+        load_rows((nc.sync,) * SCALE_ROWS, w1_plane[1], w1_scales[HALF:E, 0])
+        load_experts(w1_sb[2], w1_words, HALF, HALF)
         for half in range(2):
             load_experts(w2_sb[half], w2_words, HALF * half, HALF)
         load_packed_rows(w2s_plane, w2s_scales)
@@ -148,16 +151,19 @@ def tile_moe_shf_mlp_relu2_kernel(
             )
 
         slot_words, slot_plane = [], []
-        first = 0
-        for count in GATHER_SIZES:
+
+        def gather_slots(gathered, count, name, dtype, window, tag=None):
+            first = len(gathered)
             columns = offs_sb[:, first * C // LIST_ROWS : (first + count) * C // LIST_ROWS]
-            plane = held("slot_plane%d" % first, [P, count * C], U8)
-            words = held("slot_words%d" % first, [P, count * C], U32)
-            nc.vector.tensor_copy(plane[:], x_plane[:, 0, :].indirect(columns))
-            nc.vector.tensor_copy(words[:], x_sb[:].bitcast(U32).indirect(columns))
-            slot_plane.extend([plane[:, i * C : (i + 1) * C] for i in range(count)])
-            slot_words.extend([words[:, i * C : (i + 1) * C] for i in range(count)])
-            first = first + count
+            tile = held("%s%d" % (name, first), [P, count * C], dtype, tag)
+            nc.vector.tensor_copy(tile[:], window.indirect(columns))
+            gathered.extend([tile[:, i * C : (i + 1) * C] for i in range(count)])
+
+        for byte_count, word_counts in GATHER_SIZES:
+            last = len(slot_plane) + byte_count == E
+            gather_slots(slot_plane, byte_count, "slot_plane", U8, x_plane[:, 0, :], "slot_plane0" if last else None)
+            for count in word_counts:
+                gather_slots(slot_words, count, "slot_words", U32, x_sb[:].bitcast(U32))
 
         h_codes, h_plane, rounded, group_ending_at = [], [], [], {}
         first = 0
@@ -219,9 +225,7 @@ def tile_moe_shf_mlp_relu2_kernel(
                 in_=w2_rows_dealt[32 * q : 32 * q + 32, :, :].rearrange("p d m -> p (d m)").bitcast(I32),
             )
         load_packed_rows(w1s_plane, w1s_scales[0].rearrange("b (g n) -> g b n", g=SHARED_PASSES))
-        w1s_flat = w1s_words[0].rearrange("p l d -> p (l d)").bitcast(I32)
-        for g in range(SHARED_PASSES):
-            nc.sync.dma_start(out=w1s_sb[g][:], in_=w1s_flat[:, g * PASS : (g + 1) * PASS])
+        nc.sync.dma_start(out=w1s_sb[:], in_=w1s_words[0].rearrange("p l d -> p (l d)").bitcast(I32))
         for r, pos in enumerate((pos1, pos2)):
             nc.sync.dma_start(pos_sb[r][:], pos)
         nc.sync.dma_start(out=gate_sb[:], in_=gate.rearrange("r p t -> p r t"))
@@ -231,7 +235,7 @@ def tile_moe_shf_mlp_relu2_kernel(
             for e in range(pair, min(pair + 2, E)):
                 product(
                     slot_words[e].bitcast(FP8X4), slot_plane[e],
-                    w1_sb[e // 2][:, e % 2, :].bitcast(FP4X4), w1_plane[:, e, :], banks[e],
+                    w1_of[e].bitcast(FP4X4), w1_plane[e // HALF][:, e % HALF, :], banks[e],
                 )
             for e in range(pair, min(pair + 2, E)):
                 positive.append(relu(banks[e], "positive%d" % e, e >= FIRST_VECTOR_RELU))
@@ -263,7 +267,7 @@ def tile_moe_shf_mlp_relu2_kernel(
                 for g in range(SHARED_PASSES):
                     product(
                         x_sb[:, tokens].bitcast(FP8X4), x_plane[:, 0, tokens],
-                        w1s_sb[g][:].bitcast(FP8X4), w1s_plane[SCALE_ROWS * g :, :], banks[2 * j + g],
+                        w1s_sb[:, g * PASS : (g + 1) * PASS].bitcast(FP8X4), w1s_plane[SCALE_ROWS * g :, :], banks[2 * j + g],
                     )
                 positive_s.append(
                     [relu(banks[2 * j + g], "positive_s%d_%d" % (j, g), False) for g in range(SHARED_PASSES)]

@@ -31,6 +31,7 @@ LIST_ROWS = 16
 LINE = 8
 GATHER_SIZES = [(2, (1, 1)), (3, (2, 2)), (3, (2,))]
 W1_LOADS = [2, 2, 4]
+CODES_ON = {0: "w1_sb2"}
 QUANTIZE_SIZES = [4, 2, 1, 1]
 FIRST_VECTOR_RELU = 5
 AHEAD = 2
@@ -106,11 +107,11 @@ def tile_moe_shf_mlp_relu2_kernel(
         load_experts(w1_sb[0], w1_words, 0, 2)
         load_rows((nc.sync,) * SCALE_ROWS, w1_plane[0], w1_scales[0:HALF, 0])
         load_experts(w1_sb[1], w1_words, 2, 2)
-        nc.sync.dma_start(out=w2_rows[:].bitcast(I32), in_=w2_scales[:, 0].rearrange("e b n -> b e n").bitcast(I32))
-        load_rows((nc.sync,) * SCALE_ROWS, w1_plane[1], w1_scales[HALF:E, 0])
         load_experts(w1_sb[2], w1_words, HALF, HALF)
-        for half in range(2):
-            load_experts(w2_sb[half], w2_words, HALF * half, HALF)
+        nc.sync.dma_start(out=w2_rows[:].bitcast(I32), in_=w2_scales[:, 0].rearrange("e b n -> b e n").bitcast(I32))
+        load_experts(w2_sb[0], w2_words, 0, HALF)
+        load_rows((nc.sync,) * SCALE_ROWS, w1_plane[1], w1_scales[HALF:E, 0])
+        load_experts(w2_sb[1], w2_words, HALF, HALF)
         load_packed_rows(w2s_plane, w2s_scales)
         nc.sync.dma_start(out=w2s_sb[:], in_=w2s_words.rearrange("g p n d -> p g (n d)").bitcast(I32))
 
@@ -168,7 +169,7 @@ def tile_moe_shf_mlp_relu2_kernel(
         h_codes, h_plane, rounded, group_ending_at = [], [], [], {}
         first = 0
         for count in QUANTIZE_SIZES:
-            codes = held("h_codes%d" % first, [P, count * C], U32)
+            codes = held("h_codes%d" % first, [P, count * C], U32, CODES_ON.get(first))
             plane = held("h_plane%d" % first, [P, count * C], U8)
             values = held("rounded%d" % first, [P, count * PASS], BF16)
             h_codes.extend([codes[:, i * C : (i + 1) * C] for i in range(count)])
@@ -190,7 +191,7 @@ def tile_moe_shf_mlp_relu2_kernel(
         out_rows = out_0.rearrange("(p b) t -> p b t", p=P)
         out_words = out_1[0].rearrange("p t d -> p (t d)").bitcast(I32)
 
-        def slot_results(b, first_expert, end_expert, bank):
+        def slot_results(b, first_expert, end_expert, bank, copy):
             half = first_expert // HALF
             for e in range(first_expert, end_expert):
                 i = e % HALF
@@ -201,22 +202,23 @@ def tile_moe_shf_mlp_relu2_kernel(
                     rhs=h_codes[e].bitcast(FP8X4), rhs_scale=h_plane[e],
                     start=True, stop=True,
                 )
-            nc.scalar.copy(
-                out=y_sb[b][:, first_expert * C : end_expert * C],
-                in_=bank[:, (first_expert - HALF * half) * C : (end_expert - HALF * half) * C],
+            copy(
+                y_sb[b][:, first_expert * C : end_expert * C],
+                bank[:, (first_expert - HALF * half) * C : (end_expert - HALF * half) * C],
             )
 
-        def half_results(b, half):
-            slot_results(b, HALF * half, HALF * (half + 1), banks[4 * (b // 2) + 2 * half + b % 2])
+        def half_results(b, half, copy):
+            slot_results(b, HALF * half, HALF * (half + 1), banks[4 * (b // 2) + 2 * half + b % 2], copy)
 
-        def pick(b):
-            for r in range(2):
-                nc.vector.tensor_tensor(
-                    picked[r][:, b, :], y_sb[b][:].indirect(pos_sb[r][:]), gate_sb[:, r, :], ALU.mult
-                )
+        def pick(b, r):
+            nc.vector.tensor_tensor(picked[r][:, b, :], y_sb[b][:].indirect(pos_sb[r][:]), gate_sb[:, r, :], ALU.mult)
 
-        def shared_quantize(j):
-            nc.vector.quantize_mx(out=hs_codes[j][:].bitcast(FP8X4), scales=hs_plane[j][:], in_=rounded_s[j][:])
+        def shared_quantize(j, first_pass, end_pass):
+            words = slice(first_pass * P, end_pass * P)
+            nc.vector.quantize_mx(
+                out=hs_codes[j][:, words].bitcast(FP8X4), scales=hs_plane[j][:, words],
+                in_=rounded_s[j][:, first_pass * PASS : end_pass * PASS],
+            )
 
         deal_bytes(w2_rows_dealt, w2_rows)
         for q in range(QUADS):
@@ -251,14 +253,14 @@ def tile_moe_shf_mlp_relu2_kernel(
         for half in range(2):
             deal_fp4(half, 1)
 
-        half_results(0, 0)
-        slot_results(0, HALF, E - 1, banks[2])
-        slot_results(0, E - 1, E, banks[E - 1])
+        half_results(0, 0, nc.scalar.copy)
+        slot_results(0, HALF, E - 1, banks[2], nc.scalar.copy)
+        slot_results(0, E - 1, E, banks[E - 1], nc.scalar.copy)
         for half in range(2):
-            half_results(1, half)
+            half_results(1, half, nc.scalar.copy)
         for half in range(2):
-            half_results(2, half)
-            half_results(3, half)
+            half_results(2, half, nc.scalar.copy)
+            half_results(3, half, nc.scalar.copy)
 
         positive_s = []
         for j in range(TOKEN_TILES + 1):
@@ -279,27 +281,31 @@ def tile_moe_shf_mlp_relu2_kernel(
                     square(rounded_s[j - 1][:, g * PASS : (g + 1) * PASS], banks[2 * (j - 1) + g])
 
         for b in range(ROW_BLOCKS - 1):
-            pick(b)
+            for r in range(2):
+                pick(b, r)
         deal_bytes(w2s_plane_dealt, w2s_plane)
         nc.vector.tensor_copy(
             w2s_dealt[:].rearrange("p g d (c i) -> p g c d i", i=PACK),
             w2s_sb[:].rearrange("p g (c i d) -> p g c d i", i=PACK, d=PACK),
         )
-        shared_quantize(0)
-        pick(ROW_BLOCKS - 1)
-        for j in range(1, TOKEN_TILES):
-            shared_quantize(j)
+        shared_quantize(0, 0, SHARED_PASSES)
+        for r in range(2):
+            pick(ROW_BLOCKS - 1, r)
+        for j in range(1, TOKEN_TILES - 1):
+            shared_quantize(j, 0, SHARED_PASSES)
+        for g in range(SHARED_PASSES):
+            shared_quantize(TOKEN_TILES - 1, g, g + 1)
 
         for j in range(TOKEN_TILES):
-            for b in range(ROW_BLOCKS):
-                for g in range(SHARED_PASSES):
+            for g in range(SHARED_PASSES):
+                for b in range(ROW_BLOCKS):
                     nc.tensor.matmul_mx(
                         out=banks[YS_BANKS[j]][:, b * P : (b + 1) * P],
                         lhsT=w2s_dealt[:, g, b, :].bitcast(FP8X4),
                         lhsT_scale=w2s_plane_dealt[SCALE_ROWS * g :, b, :],
                         rhs=hs_codes[j][:, g * P : (g + 1) * P].bitcast(FP8X4),
                         rhs_scale=hs_plane[j][:, g * P : (g + 1) * P],
-                        start=(g == 0), stop=(g == SHARED_PASSES - 1),
+                        start=(g == 0 and b == 0), stop=(g == SHARED_PASSES - 1 and b == ROW_BLOCKS - 1),
                     )
 
         for j in range(TOKEN_TILES):

@@ -31,9 +31,11 @@ LIST_ROWS = 16
 LINE = 8
 GATHER_SIZES = [(2, (1, 1)), (3, (2, 2)), (3, (2,))]
 W1_LOADS = [2, 2, 4]
+SPREAD_ORDER = [0, 2, 1, 3]
 CODES_ON = {0: "w1_sb2"}
+DEALT_ON = {(1, 1): "rounded%d" % (E - 1)}
 QUANTIZE_SIZES = [4, 2, 1, 1]
-FIRST_VECTOR_RELU = 5
+VECTOR_RELUS = [4, 5, 7]
 AHEAD = 2
 YS_BANKS = [0, 4, 5, 1]
 
@@ -87,9 +89,9 @@ def tile_moe_shf_mlp_relu2_kernel(
         w2_rows_dealt = held("w2_rows_dealt", [P, PACK, P], U8)
         w1s_sb = held("w1s_sb", [P, HS], I32)
         w2s_sb = held("w2s_sb", [P, SHARED_PASSES, N], I32)
-        gate_sb = held("gate_sb", [P, 2, T], F32)
+        gate_sb = [held("gate_sb%d" % r, [P, T], F32) for r in range(2)]
         identity = held("identity", [P, P], F32)
-        w2_dealt = [[held("w2_dealt%d_%d" % (i, u), [P, HALF, 2, 2 * P], U8) for u in range(2)] for i in range(2)]
+        w2_dealt = [[], []]
         w2s_dealt = held("w2s_dealt", [P, SHARED_PASSES, PACK, P], I32)
         w2s_plane_dealt = held("w2s_plane_dealt", [P, PACK, P], U8)
 
@@ -112,13 +114,15 @@ def tile_moe_shf_mlp_relu2_kernel(
         load_experts(w2_sb[0], w2_words, 0, HALF)
         load_rows((nc.sync,) * SCALE_ROWS, w1_plane[1], w1_scales[HALF:E, 0])
         load_experts(w2_sb[1], w2_words, HALF, HALF)
-        load_packed_rows(w2s_plane, w2s_scales)
-        nc.sync.dma_start(out=w2s_sb[:], in_=w2s_words.rearrange("g p n d -> p g (n d)").bitcast(I32))
+        nc.sync.dma_start(pos_sb[0][:], pos1)
+        nc.sync.dma_start(out=gate_sb[0][:], in_=gate[0])
 
         def deal_bytes(dealt, rows):
             nc.vector.tensor_copy(dealt[:], rows[:].rearrange("p (m d) -> p d m", d=PACK))
 
         def deal_fp4(half, pair):
+            name = "w2_dealt%d_%d" % (half, pair)
+            w2_dealt[half].append(held(name, [P, HALF, 2, 2 * P], U8, DEALT_ON.get((half, pair))))
             columns = w2_sb[half][:].bitcast(U16).rearrange("p e (c i d) -> p e c d i", i=LINE, d=PACK)
             nc.vector.tensor_copy(
                 w2_dealt[half][pair][:].bitcast(U16).rearrange("p e d (c i) -> p e c d i", i=LINE),
@@ -211,7 +215,7 @@ def tile_moe_shf_mlp_relu2_kernel(
             slot_results(b, HALF * half, HALF * (half + 1), banks[4 * (b // 2) + 2 * half + b % 2], copy)
 
         def pick(b, r):
-            nc.vector.tensor_tensor(picked[r][:, b, :], y_sb[b][:].indirect(pos_sb[r][:]), gate_sb[:, r, :], ALU.mult)
+            nc.vector.tensor_tensor(picked[r][:, b, :], y_sb[b][:].indirect(pos_sb[r][:]), gate_sb[r][:], ALU.mult)
 
         def shared_quantize(j, first_pass, end_pass):
             words = slice(first_pass * P, end_pass * P)
@@ -221,16 +225,17 @@ def tile_moe_shf_mlp_relu2_kernel(
             )
 
         deal_bytes(w2_rows_dealt, w2_rows)
-        for q in range(QUADS):
+        for q in SPREAD_ORDER:
             nc.sync.dma_start(
                 out=w2_plane[32 * q : 32 * q + SCALE_ROWS, :, :].bitcast(I32),
                 in_=w2_rows_dealt[32 * q : 32 * q + 32, :, :].rearrange("p d m -> p (d m)").bitcast(I32),
             )
         load_packed_rows(w1s_plane, w1s_scales[0].rearrange("b (g n) -> g b n", g=SHARED_PASSES))
         nc.sync.dma_start(out=w1s_sb[:], in_=w1s_words[0].rearrange("p l d -> p (l d)").bitcast(I32))
-        for r, pos in enumerate((pos1, pos2)):
-            nc.sync.dma_start(pos_sb[r][:], pos)
-        nc.sync.dma_start(out=gate_sb[:], in_=gate.rearrange("r p t -> p r t"))
+        load_packed_rows(w2s_plane, w2s_scales)
+        nc.sync.dma_start(pos_sb[1][:], pos2)
+        nc.sync.dma_start(out=gate_sb[1][:], in_=gate[1])
+        nc.sync.dma_start(out=w2s_sb[:], in_=w2s_words.rearrange("g p n d -> p g (n d)").bitcast(I32))
 
         positive = []
         for pair in range(0, E + AHEAD, 2):
@@ -240,7 +245,7 @@ def tile_moe_shf_mlp_relu2_kernel(
                     w1_of[e].bitcast(FP4X4), w1_plane[e // HALF][:, e % HALF, :], banks[e],
                 )
             for e in range(pair, min(pair + 2, E)):
-                positive.append(relu(banks[e], "positive%d" % e, e >= FIRST_VECTOR_RELU))
+                positive.append(relu(banks[e], "positive%d" % e, e in VECTOR_RELUS))
             for e in range(max(pair - AHEAD, 0), pair - AHEAD + 2):
                 turn(banks[e], positive[e])
         for half in range(2):
@@ -258,9 +263,9 @@ def tile_moe_shf_mlp_relu2_kernel(
         slot_results(0, E - 1, E, banks[E - 1], nc.scalar.copy)
         for half in range(2):
             half_results(1, half, nc.scalar.copy)
-        for half in range(2):
-            half_results(2, half, nc.scalar.copy)
-            half_results(3, half, nc.scalar.copy)
+        for b in range(2, ROW_BLOCKS):
+            for half in range(2):
+                half_results(b, half, nc.scalar.copy)
 
         positive_s = []
         for j in range(TOKEN_TILES + 1):
@@ -280,24 +285,17 @@ def tile_moe_shf_mlp_relu2_kernel(
                 for g in range(SHARED_PASSES):
                     square(rounded_s[j - 1][:, g * PASS : (g + 1) * PASS], banks[2 * (j - 1) + g])
 
-        for b in range(ROW_BLOCKS - 1):
-            for r in range(2):
-                pick(b, r)
+        for b in range(ROW_BLOCKS):
+            pick(b, 0)
         deal_bytes(w2s_plane_dealt, w2s_plane)
         nc.vector.tensor_copy(
             w2s_dealt[:].rearrange("p g d (c i) -> p g c d i", i=PACK),
             w2s_sb[:].rearrange("p g (c i d) -> p g c d i", i=PACK, d=PACK),
         )
-        shared_quantize(0, 0, SHARED_PASSES)
-        for r in range(2):
-            pick(ROW_BLOCKS - 1, r)
-        for j in range(1, TOKEN_TILES - 1):
-            shared_quantize(j, 0, SHARED_PASSES)
-        for g in range(SHARED_PASSES):
-            shared_quantize(TOKEN_TILES - 1, g, g + 1)
 
-        for j in range(TOKEN_TILES):
-            for g in range(SHARED_PASSES):
+        def shared_passes(j, first_pass, end_pass):
+            shared_quantize(j, first_pass, end_pass)
+            for g in range(first_pass, end_pass):
                 for b in range(ROW_BLOCKS):
                     nc.tensor.matmul_mx(
                         out=banks[YS_BANKS[j]][:, b * P : (b + 1) * P],
@@ -308,22 +306,25 @@ def tile_moe_shf_mlp_relu2_kernel(
                         start=(g == 0 and b == 0), stop=(g == SHARED_PASSES - 1 and b == ROW_BLOCKS - 1),
                     )
 
-        for j in range(TOKEN_TILES):
+        def add_picks(j):
             tokens = slice(j * P, (j + 1) * P)
             nc.vector.tensor_tensor(routed[j][:], picked[0][:, :, tokens], picked[1][:, :, tokens], ALU.add)
-        for j in range(TOKEN_TILES):
-            tokens = slice(j * P, (j + 1) * P)
+
+        def add_shared(j):
             nc.vector.tensor_tensor(
                 result[j][:], banks[YS_BANKS[j]][:], routed[j][:].rearrange("p b t -> p (b t)"), ALU.add
             )
-            nc.sync.dma_start(out=out_rows[:, :, tokens], in_=result[j][:].rearrange("p (b t) -> p b t", b=ROW_BLOCKS))
-            woven = grouped[j][:].rearrange("p (c i b) -> p c b i", i=PACK, b=PACK)
-            rows = result[j][:].rearrange("p (b c i) -> p c b i", i=PACK, b=PACK)
-            if j == TOKEN_TILES - 1:
-                nc.vector.tensor_copy(woven, rows)
-            else:
-                nc.scalar.copy(out=woven, in_=rows)
-        for j in range(TOKEN_TILES):
+            nc.sync.dma_start(
+                out=out_rows[:, :, j * P : (j + 1) * P], in_=result[j][:].rearrange("p (b t) -> p b t", b=ROW_BLOCKS)
+            )
+
+        def weave(j, copy):
+            copy(
+                grouped[j][:].rearrange("p (c i b) -> p c b i", i=PACK, b=PACK),
+                result[j][:].rearrange("p (b c i) -> p c b i", i=PACK, b=PACK),
+            )
+
+        def out_quantize(j):
             tokens = slice(j * P, (j + 1) * P)
             nc.vector.quantize_mx(
                 out=out_codes[:, tokens].bitcast(FP8X4), scales=out_plane[:, tokens], in_=grouped[j][:]
@@ -331,6 +332,31 @@ def tile_moe_shf_mlp_relu2_kernel(
             if j % 2 == 1:
                 both_tiles = slice((j - 1) * P, (j + 1) * P)
                 nc.sync.dma_start(out=out_words[:, both_tiles], in_=out_codes[:, both_tiles].bitcast(I32))
+
+        for b in range(2):
+            pick(b, 1)
+        shared_passes(0, 0, SHARED_PASSES)
+        for b in range(2, ROW_BLOCKS):
+            pick(b, 1)
+        shared_passes(1, 0, SHARED_PASSES)
+        add_picks(0)
+        add_picks(1)
+        add_shared(0)
+        shared_passes(2, 0, SHARED_PASSES)
+        add_picks(2)
+        shared_passes(3, 0, 1)
+        add_shared(1)
+        shared_passes(3, 1, 2)
+        add_picks(3)
+        add_shared(2)
+        for j in range(TOKEN_TILES - 1):
+            weave(j, nc.scalar.copy)
+        out_quantize(0)
+        add_shared(3)
+        out_quantize(1)
+        weave(3, nc.vector.tensor_copy)
+        out_quantize(2)
+        out_quantize(3)
         for q in range(QUADS):
             (nc.sync, nc.scalar)[q % 2].dma_start(
                 out=out_2[0, SCALE_ROWS * q : SCALE_ROWS * (q + 1), :].bitcast(I32),

@@ -29,11 +29,12 @@ SHARED_PASSES = HS // PASS
 HALF = E // 2
 LIST_ROWS = 16
 LINE = 8
-GATHER_SIZES = [(2, (1, 1)), (3, (2, 2)), (3, (2,))]
+GATHER_SIZES = [(4, (1, 1, 2)), (4, (2, 2))]
+SPARE = 256
 W1_LOADS = [2, 2, 4]
 SPREAD_ORDER = [0, 2, 1, 3]
 CODES_ON = {0: "w1_sb2"}
-DEALT_ON = {(1, 1): "rounded%d" % (E - 1)}
+DEALT_ON = {}
 QUANTIZE_SIZES = [4, 2, 1, 1]
 VECTOR_RELUS = [4, 5, 7]
 AHEAD = 2
@@ -77,7 +78,7 @@ def tile_moe_shf_mlp_relu2_kernel(
         offs_sb = keep.tile([P, SLOTS // LIST_ROWS], U16, name="offs_sb")
         pos_sb = [keep.tile([P, T // LIST_ROWS], U16, name="pos%d_sb" % r) for r in range(2)]
         x_sb = held("x_sb", [P, T], I32)
-        x_plane = held("x_plane", [P, 1, T], U8)
+        x_plane = held("x_plane", [P, 1, T + SPARE], U8)
         w1_plane = [held("w1_plane%d" % i, [P, HALF, H], U8) for i in range(2)]
         w2_plane = held("w2_plane", [P, E, N], U8)
         w1s_plane = held("w1s_plane", [P, PASS], U8)
@@ -95,16 +96,21 @@ def tile_moe_shf_mlp_relu2_kernel(
         w2s_dealt = held("w2s_dealt", [P, SHARED_PASSES, PACK, P], I32)
         w2s_plane_dealt = held("w2s_plane_dealt", [P, PACK, P], U8)
 
-        nc.gpsimd.memset(x_plane[:].bitcast(I32), 0)
-        for half in range(2):
-            nc.vector.memset(w1_plane[half][:].bitcast(I32), 0)
+        nc.gpsimd.memset(x_plane[:, 0, T : T + SPARE].bitcast(I32), 0)
+        nc.vector.memset(w1_plane[0][:].bitcast(I32), 0)
         nc.vector.memset(w2_plane[:].bitcast(I32), 0)
+        nc.gpsimd.memset(w1_plane[1][:].bitcast(I32), 0)
         make_identity(nc, identity[:])
         nc.gpsimd.memset(w2s_plane[:].bitcast(I32), 0)
         nc.gpsimd.memset(w1s_plane[:].bitcast(I32), 0)
 
         nc.sync.dma_start(offs_sb[:], offs)
-        load_rows((nc.sync, nc.sync, nc.scalar, nc.scalar), x_plane, x_scales)
+        for q in range(QUADS):
+            rows = x_scales[0, SCALE_ROWS * q : SCALE_ROWS * (q + 1), :].bitcast(I32)
+            (nc.sync, nc.sync, nc.scalar, nc.scalar)[q].dma_start(
+                out=x_plane[32 * q : 32 * (q + 1), 0, 0:T].bitcast(I32),
+                in_=rows.unsqueeze(0).to_broadcast([32 // SCALE_ROWS, SCALE_ROWS, T // 4]),
+            )
         nc.sync.dma_start(out=x_sb[:], in_=x_words[0].rearrange("p t d -> p (t d)").bitcast(I32))
         load_experts(w1_sb[0], w1_words, 0, 2)
         load_rows((nc.sync,) * SCALE_ROWS, w1_plane[0], w1_scales[0:HALF, 0])
@@ -166,7 +172,7 @@ def tile_moe_shf_mlp_relu2_kernel(
 
         for byte_count, word_counts in GATHER_SIZES:
             last = len(slot_plane) + byte_count == E
-            gather_slots(slot_plane, byte_count, "slot_plane", U8, x_plane[:, 0, :], "slot_plane0" if last else None)
+            gather_slots(slot_plane, byte_count, "slot_plane", U8, x_plane[:, 0, :], "slot_words1" if last else None)
             for count in word_counts:
                 gather_slots(slot_words, count, "slot_words", U32, x_sb[:].bitcast(U32))
 
@@ -230,12 +236,12 @@ def tile_moe_shf_mlp_relu2_kernel(
                 out=w2_plane[32 * q : 32 * q + SCALE_ROWS, :, :].bitcast(I32),
                 in_=w2_rows_dealt[32 * q : 32 * q + 32, :, :].rearrange("p d m -> p (d m)").bitcast(I32),
             )
+        nc.sync.dma_start(out=w2s_sb[:], in_=w2s_words.rearrange("g p n d -> p g (n d)").bitcast(I32))
         load_packed_rows(w1s_plane, w1s_scales[0].rearrange("b (g n) -> g b n", g=SHARED_PASSES))
         nc.sync.dma_start(out=w1s_sb[:], in_=w1s_words[0].rearrange("p l d -> p (l d)").bitcast(I32))
         load_packed_rows(w2s_plane, w2s_scales)
         nc.sync.dma_start(pos_sb[1][:], pos2)
         nc.sync.dma_start(out=gate_sb[1][:], in_=gate[1])
-        nc.sync.dma_start(out=w2s_sb[:], in_=w2s_words.rearrange("g p n d -> p g (n d)").bitcast(I32))
 
         positive = []
         for pair in range(0, E + AHEAD, 2):
@@ -257,6 +263,11 @@ def tile_moe_shf_mlp_relu2_kernel(
                     nc.vector.quantize_mx(out=codes[:].bitcast(FP8X4), scales=plane[:], in_=values[:])
         for half in range(2):
             deal_fp4(half, 1)
+
+        nc.vector.tensor_copy(
+            w2s_dealt[:].rearrange("p g d (c i) -> p g c d i", i=PACK),
+            w2s_sb[:].rearrange("p g (c i d) -> p g c d i", i=PACK, d=PACK),
+        )
 
         half_results(0, 0, nc.scalar.copy)
         slot_results(0, HALF, E - 1, banks[2], nc.scalar.copy)
@@ -288,10 +299,6 @@ def tile_moe_shf_mlp_relu2_kernel(
         for b in range(ROW_BLOCKS):
             pick(b, 0)
         deal_bytes(w2s_plane_dealt, w2s_plane)
-        nc.vector.tensor_copy(
-            w2s_dealt[:].rearrange("p g d (c i) -> p g c d i", i=PACK),
-            w2s_sb[:].rearrange("p g (c i d) -> p g c d i", i=PACK, d=PACK),
-        )
 
         def shared_passes(j, first_pass, end_pass):
             shared_quantize(j, first_pass, end_pass)

from contextlib import ExitStack

import concourse.mybir as mybir
from concourse.masks import make_identity

K, T, E, C, H, HS, N = 512, 512, 8, 128, 512, 1024, 512
FLOPS = 2 * (E * C * (K * H + H * N) + T * (K * HS + HS * N))

F32 = mybir.dt.float32
BF16 = mybir.dt.bfloat16
I32 = mybir.dt.int32
U32 = mybir.dt.uint32
U16 = mybir.dt.uint16
U8 = mybir.dt.uint8
FP8X4 = mybir.dt.float8_e4m3fn_x4
FP4X4 = mybir.dt.float4_e2m1fn_x4
ACT = mybir.ActivationFunctionType
ALU = mybir.AluOpType

P = 128
PACK = 4
QUADS = 4
SCALE_ROWS = 4
PASS = P * PACK
SLOTS = E * C
ROW_BLOCKS = N // P
TOKEN_TILES = T // P
SHARED_PASSES = HS // PASS
HALF = E // 2
LIST_ROWS = 16
LINE = 8
GATHER_SIZES = [(4, (1, 1, 2)), (4, (2, 2))]
SPARE = 256
W1_LOADS = [2, 2, 4]
SPREAD_ORDER = [0, 2, 1, 3]
CODES_ON = {0: "w1_sb2"}
DEALT_ON = {}
QUANTIZE_SIZES = [4, 2, 1, 1]
VECTOR_RELUS = [4, 5, 7]
AHEAD = 2
YS_BANKS = [0, 4, 5, 1]


def tile_moe_shf_mlp_relu2_kernel(
    tc, x_words, x_scales, w1_words, w1_scales, w2_words, w2_scales, w1s_words, w1s_scales,
    w2s_words, w2s_scales, gate, offs, pos1, pos2, out_0, out_1, out_2,
):
    nc = tc.nc
    with ExitStack() as ctx:
        keep = ctx.enter_context(tc.tile_pool(name="keep", bufs=1))
        psum = ctx.enter_context(tc.psum_pool(name="psum", bufs=1))

        def held(name, shape, dtype, tag=None):
            return keep.tile(shape, dtype, name=name, tag=tag or name, align_bytes=64)

        banks = [psum.tile([P, PASS], F32, name="bank%d" % i) for i in range(8)]

        def load_rows(queues, plane, scales):
            for r in range(SCALE_ROWS):
                queues[r].dma_start(
                    out=plane[r:P:32, :, :].bitcast(I32),
                    in_=scales[:, r:16:SCALE_ROWS, :].rearrange("g q n -> q g n").bitcast(I32),
                )

        def load_packed_rows(plane, scales):
            for q in range(QUADS):
                nc.sync.dma_start(
                    out=plane[32 * q : 32 * q + SCALE_ROWS * SHARED_PASSES, :].bitcast(I32),
                    in_=scales[:, SCALE_ROWS * q : SCALE_ROWS * (q + 1), :].bitcast(I32),
                )

        def load_experts(tile, words, first, count):
            nc.sync.dma_start(
                out=tile[:].bitcast(I32),
                in_=words[first : first + count, 0].rearrange("e p n -> p e n").bitcast(I32),
            )

        offs_sb = keep.tile([P, SLOTS // LIST_ROWS], U16, name="offs_sb")
        pos_sb = [keep.tile([P, T // LIST_ROWS], U16, name="pos%d_sb" % r) for r in range(2)]
        x_sb = held("x_sb", [P, T], I32)
        x_plane = held("x_plane", [P, 1, T + SPARE], U8)
        w1_plane = [held("w1_plane%d" % i, [P, HALF, H], U8) for i in range(2)]
        w2_plane = held("w2_plane", [P, E, N], U8)
        w1s_plane = held("w1s_plane", [P, PASS], U8)
        w2s_plane = held("w2s_plane", [P, N], U8)
        w1_sb = [held("w1_sb%d" % i, [P, count, 2 * H], U8) for i, count in enumerate(W1_LOADS)]
        w1_of = [w1_sb[i][:, u, :] for i, count in enumerate(W1_LOADS) for u in range(count)]
        w2_sb = [held("w2_sb%d" % i, [P, HALF, 2 * N], U8) for i in range(2)]
        w2_rows = held("w2_rows", [P, N], U8)
        w2_rows_dealt = held("w2_rows_dealt", [P, PACK, P], U8)
        w1s_sb = held("w1s_sb", [P, HS], I32)
        w2s_sb = held("w2s_sb", [P, SHARED_PASSES, N], I32)
        gate_sb = [held("gate_sb%d" % r, [P, T], F32) for r in range(2)]
        identity = held("identity", [P, P], F32)
        w2_dealt = [[], []]
        w2s_dealt = held("w2s_dealt", [P, SHARED_PASSES, PACK, P], I32)
        w2s_plane_dealt = held("w2s_plane_dealt", [P, PACK, P], U8)

        nc.gpsimd.memset(x_plane[:, 0, T : T + SPARE].bitcast(I32), 0)
        nc.vector.memset(w1_plane[0][:].bitcast(I32), 0)
        nc.vector.memset(w2_plane[:].bitcast(I32), 0)
        nc.gpsimd.memset(w1_plane[1][:].bitcast(I32), 0)
        make_identity(nc, identity[:])
        nc.gpsimd.memset(w2s_plane[:].bitcast(I32), 0)
        nc.gpsimd.memset(w1s_plane[:].bitcast(I32), 0)

        nc.sync.dma_start(offs_sb[:], offs)
        for q in range(QUADS):
            rows = x_scales[0, SCALE_ROWS * q : SCALE_ROWS * (q + 1), :].bitcast(I32)
            (nc.sync, nc.sync, nc.scalar, nc.scalar)[q].dma_start(
                out=x_plane[32 * q : 32 * (q + 1), 0, 0:T].bitcast(I32),
                in_=rows.unsqueeze(0).to_broadcast([32 // SCALE_ROWS, SCALE_ROWS, T // 4]),
            )
        nc.sync.dma_start(out=x_sb[:], in_=x_words[0].rearrange("p t d -> p (t d)").bitcast(I32))
        load_experts(w1_sb[0], w1_words, 0, 2)
        load_rows((nc.sync,) * SCALE_ROWS, w1_plane[0], w1_scales[0:HALF, 0])
        load_experts(w1_sb[1], w1_words, 2, 2)
        load_experts(w1_sb[2], w1_words, HALF, HALF)
        nc.sync.dma_start(out=w2_rows[:].bitcast(I32), in_=w2_scales[:, 0].rearrange("e b n -> b e n").bitcast(I32))
        load_experts(w2_sb[0], w2_words, 0, HALF)
        load_rows((nc.sync,) * SCALE_ROWS, w1_plane[1], w1_scales[HALF:E, 0])
        load_experts(w2_sb[1], w2_words, HALF, HALF)
        nc.sync.dma_start(pos_sb[0][:], pos1)
        nc.sync.dma_start(out=gate_sb[0][:], in_=gate[0])

        def deal_bytes(dealt, rows):
            nc.vector.tensor_copy(dealt[:], rows[:].rearrange("p (m d) -> p d m", d=PACK))

        def deal_fp4(half, pair):
            name = "w2_dealt%d_%d" % (half, pair)
            w2_dealt[half].append(held(name, [P, HALF, 2, 2 * P], U8, DEALT_ON.get((half, pair))))
            columns = w2_sb[half][:].bitcast(U16).rearrange("p e (c i d) -> p e c d i", i=LINE, d=PACK)
            nc.vector.tensor_copy(
                w2_dealt[half][pair][:].bitcast(U16).rearrange("p e d (c i) -> p e c d i", i=LINE),
                columns[:, :, :, 2 * pair : 2 * pair + 2, :],
            )

        def product(tokens, token_scales, weights, weight_scales, bank):
            nc.tensor.matmul_mx(
                out=bank[:], lhsT=tokens, lhsT_scale=token_scales, rhs=weights, rhs_scale=weight_scales,
                start=True, stop=True,
            )

        def relu(bank, name, on_vector):
            positive = held(name, [P, PASS], F32)
            dealt = bank[:].rearrange("p (m d) -> p d m", d=PACK)
            target = positive[:].rearrange("p (d m) -> p d m", d=PACK)
            if on_vector:
                nc.vector.tensor_scalar(out=target, in0=dealt, scalar1=0.0, scalar2=None, op0=ALU.max)
            else:
                nc.scalar.activation(out=target, in_=dealt, func=ACT.Relu)
            return positive

        def turn(bank, positive):
            for d in range(PACK):
                nc.tensor.transpose(bank[:, d * P : (d + 1) * P], positive[:, d * P : (d + 1) * P], identity[:])

        def square(target, bank):
            nc.scalar.activation(
                out=target.rearrange("p (s d) -> p s d", d=PACK),
                in_=bank[:].rearrange("p (d s) -> p s d", d=PACK), func=ACT.Square,
            )

        slot_words, slot_plane = [], []

        def gather_slots(gathered, count, name, dtype, window, tag=None):
            first = len(gathered)
            columns = offs_sb[:, first * C // LIST_ROWS : (first + count) * C // LIST_ROWS]
            tile = held("%s%d" % (name, first), [P, count * C], dtype, tag)
            nc.vector.tensor_copy(tile[:], window.indirect(columns))
            gathered.extend([tile[:, i * C : (i + 1) * C] for i in range(count)])

        for byte_count, word_counts in GATHER_SIZES:
            last = len(slot_plane) + byte_count == E
            gather_slots(slot_plane, byte_count, "slot_plane", U8, x_plane[:, 0, :], "slot_words1" if last else None)
            for count in word_counts:
                gather_slots(slot_words, count, "slot_words", U32, x_sb[:].bitcast(U32))

        h_codes, h_plane, rounded, group_ending_at = [], [], [], {}
        first = 0
        for count in QUANTIZE_SIZES:
            codes = held("h_codes%d" % first, [P, count * C], U32, CODES_ON.get(first))
            plane = held("h_plane%d" % first, [P, count * C], U8)
            values = held("rounded%d" % first, [P, count * PASS], BF16)
            h_codes.extend([codes[:, i * C : (i + 1) * C] for i in range(count)])
            h_plane.extend([plane[:, i * C : (i + 1) * C] for i in range(count)])
            rounded.extend([values[:, i * PASS : (i + 1) * PASS] for i in range(count)])
            first = first + count
            group_ending_at.setdefault(first - 1, (codes, plane, values))

        y_sb = [held("y_sb%d" % b, [P, SLOTS], F32) for b in range(ROW_BLOCKS)]
        picked = [held("picked%d" % r, [P, ROW_BLOCKS, T], F32) for r in range(2)]
        rounded_s = [held("rounded_s%d" % j, [P, SHARED_PASSES * PASS], BF16) for j in range(TOKEN_TILES)]
        hs_codes = [held("hs_codes%d" % j, [P, SHARED_PASSES * P], U32) for j in range(TOKEN_TILES)]
        hs_plane = [held("hs_plane%d" % j, [P, SHARED_PASSES * P], U8) for j in range(TOKEN_TILES)]
        out_codes = held("out_codes", [P, T], U32)
        out_plane = held("out_plane", [P, T], U8)
        routed = [held("routed%d" % j, [P, ROW_BLOCKS, P], F32) for j in range(TOKEN_TILES)]
        result = [held("result%d" % j, [P, ROW_BLOCKS * P], F32) for j in range(TOKEN_TILES)]
        grouped = [held("grouped%d" % j, [P, PACK * P], BF16) for j in range(TOKEN_TILES)]
        out_rows = out_0.rearrange("(p b) t -> p b t", p=P)
        out_words = out_1[0].rearrange("p t d -> p (t d)").bitcast(I32)

        def slot_results(b, first_expert, end_expert, bank, copy):
            half = first_expert // HALF
            for e in range(first_expert, end_expert):
                i = e % HALF
                nc.tensor.matmul_mx(
                    out=bank[:, i * C : (i + 1) * C],
                    lhsT=w2_dealt[half][b // 2][:, i, b % 2, :].bitcast(FP4X4),
                    lhsT_scale=w2_plane[:, e, b * P : (b + 1) * P],
                    rhs=h_codes[e].bitcast(FP8X4), rhs_scale=h_plane[e],
                    start=True, stop=True,
                )
            copy(
                y_sb[b][:, first_expert * C : end_expert * C],
                bank[:, (first_expert - HALF * half) * C : (end_expert - HALF * half) * C],
            )

        def half_results(b, half, copy):
            slot_results(b, HALF * half, HALF * (half + 1), banks[4 * (b // 2) + 2 * half + b % 2], copy)

        def pick(b, r):
            nc.vector.tensor_tensor(picked[r][:, b, :], y_sb[b][:].indirect(pos_sb[r][:]), gate_sb[r][:], ALU.mult)

        def shared_quantize(j, first_pass, end_pass):
            words = slice(first_pass * P, end_pass * P)
            nc.vector.quantize_mx(
                out=hs_codes[j][:, words].bitcast(FP8X4), scales=hs_plane[j][:, words],
                in_=rounded_s[j][:, first_pass * PASS : end_pass * PASS],
            )

        deal_bytes(w2_rows_dealt, w2_rows)
        for q in SPREAD_ORDER:
            nc.sync.dma_start(
                out=w2_plane[32 * q : 32 * q + SCALE_ROWS, :, :].bitcast(I32),
                in_=w2_rows_dealt[32 * q : 32 * q + 32, :, :].rearrange("p d m -> p (d m)").bitcast(I32),
            )
        nc.sync.dma_start(out=w2s_sb[:], in_=w2s_words.rearrange("g p n d -> p g (n d)").bitcast(I32))
        load_packed_rows(w1s_plane, w1s_scales[0].rearrange("b (g n) -> g b n", g=SHARED_PASSES))
        nc.sync.dma_start(out=w1s_sb[:], in_=w1s_words[0].rearrange("p l d -> p (l d)").bitcast(I32))
        load_packed_rows(w2s_plane, w2s_scales)
        nc.sync.dma_start(pos_sb[1][:], pos2)
        nc.sync.dma_start(out=gate_sb[1][:], in_=gate[1])

        positive = []
        for pair in range(0, E + AHEAD, 2):
            for e in range(pair, min(pair + 2, E)):
                product(
                    slot_words[e].bitcast(FP8X4), slot_plane[e],
                    w1_of[e].bitcast(FP4X4), w1_plane[e // HALF][:, e % HALF, :], banks[e],
                )
            for e in range(pair, min(pair + 2, E)):
                positive.append(relu(banks[e], "positive%d" % e, e in VECTOR_RELUS))
            for e in range(max(pair - AHEAD, 0), pair - AHEAD + 2):
                turn(banks[e], positive[e])
        for half in range(2):
            deal_fp4(half, 0)
            for e in range(HALF * half, HALF * (half + 1)):
                square(rounded[e], banks[e])
                if e in group_ending_at:
                    codes, plane, values = group_ending_at[e]
                    nc.vector.quantize_mx(out=codes[:].bitcast(FP8X4), scales=plane[:], in_=values[:])
        for half in range(2):
            deal_fp4(half, 1)

        nc.vector.tensor_copy(
            w2s_dealt[:].rearrange("p g d (c i) -> p g c d i", i=PACK),
            w2s_sb[:].rearrange("p g (c i d) -> p g c d i", i=PACK, d=PACK),
        )

        half_results(0, 0, nc.scalar.copy)
        slot_results(0, HALF, E - 1, banks[2], nc.scalar.copy)
        slot_results(0, E - 1, E, banks[E - 1], nc.scalar.copy)
        for half in range(2):
            half_results(1, half, nc.scalar.copy)
        for b in range(2, ROW_BLOCKS):
            for half in range(2):
                half_results(b, half, nc.scalar.copy)

        positive_s = []
        for j in range(TOKEN_TILES + 1):
            if j < TOKEN_TILES:
                tokens = slice(j * P, (j + 1) * P)
                for g in range(SHARED_PASSES):
                    product(
                        x_sb[:, tokens].bitcast(FP8X4), x_plane[:, 0, tokens],
                        w1s_sb[:, g * PASS : (g + 1) * PASS].bitcast(FP8X4), w1s_plane[SCALE_ROWS * g :, :], banks[2 * j + g],
                    )
                positive_s.append(
                    [relu(banks[2 * j + g], "positive_s%d_%d" % (j, g), False) for g in range(SHARED_PASSES)]
                )
            if j > 0:
                for g in range(SHARED_PASSES):
                    turn(banks[2 * (j - 1) + g], positive_s[j - 1][g])
                for g in range(SHARED_PASSES):
                    square(rounded_s[j - 1][:, g * PASS : (g + 1) * PASS], banks[2 * (j - 1) + g])

        for b in range(ROW_BLOCKS):
            pick(b, 0)
        deal_bytes(w2s_plane_dealt, w2s_plane)

        def shared_passes(j, first_pass, end_pass):
            shared_quantize(j, first_pass, end_pass)
            for g in range(first_pass, end_pass):
                for b in range(ROW_BLOCKS):
                    nc.tensor.matmul_mx(
                        out=banks[YS_BANKS[j]][:, b * P : (b + 1) * P],
                        lhsT=w2s_dealt[:, g, b, :].bitcast(FP8X4),
                        lhsT_scale=w2s_plane_dealt[SCALE_ROWS * g :, b, :],
                        rhs=hs_codes[j][:, g * P : (g + 1) * P].bitcast(FP8X4),
                        rhs_scale=hs_plane[j][:, g * P : (g + 1) * P],
                        start=(g == 0 and b == 0), stop=(g == SHARED_PASSES - 1 and b == ROW_BLOCKS - 1),
                    )

        def add_picks(j):
            tokens = slice(j * P, (j + 1) * P)
            nc.vector.tensor_tensor(routed[j][:], picked[0][:, :, tokens], picked[1][:, :, tokens], ALU.add)

        def add_shared(j):
            nc.vector.tensor_tensor(
                result[j][:], banks[YS_BANKS[j]][:], routed[j][:].rearrange("p b t -> p (b t)"), ALU.add
            )
            nc.sync.dma_start(
                out=out_rows[:, :, j * P : (j + 1) * P], in_=result[j][:].rearrange("p (b t) -> p b t", b=ROW_BLOCKS)
            )

        def weave(j, copy):
            copy(
                grouped[j][:].rearrange("p (c i b) -> p c b i", i=PACK, b=PACK),
                result[j][:].rearrange("p (b c i) -> p c b i", i=PACK, b=PACK),
            )

        def out_quantize(j):
            tokens = slice(j * P, (j + 1) * P)
            nc.vector.quantize_mx(
                out=out_codes[:, tokens].bitcast(FP8X4), scales=out_plane[:, tokens], in_=grouped[j][:]
            )
            if j % 2 == 1:
                both_tiles = slice((j - 1) * P, (j + 1) * P)
                nc.sync.dma_start(out=out_words[:, both_tiles], in_=out_codes[:, both_tiles].bitcast(I32))

        for b in range(2):
            pick(b, 1)
        shared_passes(0, 0, SHARED_PASSES)
        for b in range(2, ROW_BLOCKS):
            pick(b, 1)
        shared_passes(1, 0, SHARED_PASSES)
        add_picks(0)
        add_picks(1)
        add_shared(0)
        shared_passes(2, 0, SHARED_PASSES)
        add_picks(2)
        shared_passes(3, 0, 1)
        add_shared(1)
        shared_passes(3, 1, 2)
        add_picks(3)
        add_shared(2)
        for j in range(TOKEN_TILES - 1):
            weave(j, nc.scalar.copy)
        out_quantize(0)
        add_shared(3)
        out_quantize(1)
        weave(3, nc.vector.tensor_copy)
        out_quantize(2)
        out_quantize(3)
        for q in range(QUADS):
            (nc.sync, nc.scalar)[q % 2].dma_start(
                out=out_2[0, SCALE_ROWS * q : SCALE_ROWS * (q + 1), :].bitcast(I32),
                in_=out_plane[32 * q : 32 * q + SCALE_ROWS, :].bitcast(I32),
            )
